import numpy as np
import ml_dtypes


def mxq(x, axis, fmt="e4m3"):
    dtype, down = {"e4m3": (ml_dtypes.float8_e4m3fn, 7), "e5m2": (ml_dtypes.float8_e5m2, 14)}[fmt]
    v = np.moveaxis(np.asarray(x, np.float32).astype(ml_dtypes.bfloat16).astype(np.float64), axis, -1)
    blocks = v.reshape(v.shape[:-1] + (-1, 32))
    amax = np.abs(blocks).max(-1, keepdims=True)
    byte = np.maximum(np.where(amax > 0, np.frexp(amax)[1] - 1 + 127, 0) - down, 1)
    scale = np.exp2(byte - 127.0)
    codes = (blocks / scale).astype(np.float32).astype(dtype).astype(np.float64)
    return np.moveaxis((codes * scale).reshape(v.shape), -1, axis)


WIDE = False


def mx_kscale(k):
    if not WIDE:
        return np.ones(k)
    levels = np.array([10, -10, 5, -5, 0])
    if k % 512:
        return np.exp2(np.random.permutation(np.resize(levels, k // 32))).repeat(32)
    a = np.empty((k // 512, 16))
    for p in range(k // 512):
        a[p, :8] = np.random.permutation(np.resize(levels, 8))
        for g in range(8):
            far = levels[np.abs(levels - a[p, g]) >= 10]
            a[p, g + 8] = far[np.random.randint(len(far))]
    return np.exp2(a.ravel()).repeat(32)


def f64(x):
    return np.asarray(x).astype(np.float64)


def striped(idx):
    return np.tile(np.asarray(idx).reshape(-1, 16).T, (8, 1)).astype(np.uint16)


def unstriped(offs):
    return offs[:16].T.reshape(-1).astype(np.int64)


E2M1 = np.array([0.0, 0.5, 1.0, 1.5, 2.0, 3.0, 4.0, 6.0, -0.0, -0.5, -1.0, -1.5, -2.0, -3.0, -4.0, -6.0])


def pack_weight(w, fmt):
    k, n = w.shape
    w = f64(np.asarray(w, np.float32).astype(ml_dtypes.bfloat16)).reshape(k // 32, 32, n)
    amax = np.abs(w).max(1)
    if fmt == "e4m3":
        byte = np.frexp(amax)[1] - 1 + 127 - 7
    else:
        mant, ex = np.frexp(amax / 6.0)
        byte = np.where(mant > 0.5, ex, ex - 1) + 127
    byte = np.clip(np.where(amax > 0, byte, 1), 1, 254)
    scaled = (w * np.exp2(127.0 - byte)[:, None, :]).reshape(k, n).astype(np.float32)
    by_word = np.ascontiguousarray(scaled.reshape(k // 512, 128, 4, n).transpose(0, 1, 3, 2))
    if fmt == "e4m3":
        words = by_word.astype(ml_dtypes.float8_e4m3fn).view(np.uint8)
    else:
        c = by_word.astype(ml_dtypes.float4_e2m1fn).view(np.uint8) & 0xF
        words = (c[..., 0::2] | (c[..., 1::2] << 4)).reshape(k // 512, 128, 2 * n)
    return np.ascontiguousarray(words), np.ascontiguousarray(byte.astype(np.uint8).reshape(k // 512, 16, n))


def unpack_weight(words, scales, fmt):
    g, _, n = scales.shape
    words = np.ascontiguousarray(words).reshape(g, 128, n, -1)
    if fmt == "e4m3":
        vals = words.view(ml_dtypes.float8_e4m3fn).astype(np.float64)
    else:
        nib = np.empty((g, 128, n, 4), np.uint8)
        nib[..., 0::2] = words & 0xF
        nib[..., 1::2] = words >> 4
        vals = E2M1[nib]
    vals = vals * np.repeat(np.exp2(scales.astype(np.float64) - 127.0), 8, axis=1)[..., None]
    return vals.transpose(0, 1, 3, 2).reshape(g * 512, n)


B, N, T, D, NQ = 1, 1024, 4096, 1024, 128
SEG = 32


def setup_inputs():
    n = np.random.standard_normal
    pages = np.random.permutation(T // 32)[:B * N // 32]
    idx = (pages[:, None] * 32 + np.arange(32)[None, :]).reshape(-1)
    s = mx_kscale(D)[:, None]
    kp = pack_weight(n((D, T)) / s, "e2m1")
    return {
        "qT": (n((B, D, NQ)) * s * (1.00 / np.sqrt(D))).astype(np.float32),
        "k_words": np.ascontiguousarray(kp[0].reshape(1, 2, 128, T, 2).transpose(0, 2, 3, 1, 4)).reshape(1, 128, T, 4),
        "k_scales": kp[1],
        "kb": np.tile(n(4096), (128, 1)).astype(np.float32),
        "pw": (np.random.uniform(0.5, 1.5, (B, NQ, 1))).astype(np.float32),
        "offs": striped(idx),
    }


def reference(qT, k_words, k_scales, kb, pw, offs):
    idx = unstriped(offs)
    pick = lambda x, which: x[:, which].reshape(x.shape[0], B, -1).transpose(1, 0, 2)
    k = unpack_weight(k_words.reshape(1, 128, T, 2, 2).transpose(0, 3, 1, 2, 4).reshape(2, 128, 2 * T), k_scales, "e2m1")
    kg = pick(k, idx)
    qq = mxq(f64(qT), 1, "e4m3")
    a = qq.transpose(0, 2, 1) @ kg
    y = (a + pick(f64(kb), idx)[:, :1, :]).reshape(B, NQ, N // SEG, SEG).max(-1) * f64(pw)
    return y

@@ -1,0 +1,154 @@
+from contextlib import ExitStack
+
+import concourse.mybir as mybir
+from concourse.masks import make_identity
+
+F32 = mybir.dt.float32
+BF16 = mybir.dt.bfloat16
+I32 = mybir.dt.int32
+U32 = mybir.dt.uint32
+U16 = mybir.dt.uint16
+U8 = mybir.dt.uint8
+FP8X4 = mybir.dt.float8_e4m3fn_x4
+FP4X4 = mybir.dt.float4_e2m1fn_x4
+
+P = 128
+T = 4096
+N = 1024
+NQ = 128
+SEG = 32
+HALF = 512
+PASSES = 2
+KP = 512
+
+FLOPS = 2 * 1024 * N * NQ
+BYTES = P * T * 4 + 32 * T + 1024 * NQ * 4 + T * 4 + NQ * 4 + P * 64 * 2 + NQ * 32 * 4
+
+
+def tile_attend_page_prior_kernel(tc, qT, k_words, k_scales, kb, pw, offs, out):
+    nc = tc.nc
+    add = mybir.AluOpType.add
+    amax = mybir.AluOpType.max
+    with ExitStack() as ctx:
+        keep = ctx.enter_context(tc.tile_pool(name="keep", bufs=1))
+        psum = ctx.enter_context(tc.psum_pool(name="psum", bufs=1))
+
+        offsets = keep.tile([P, N // 16], U16, name="offsets")
+        word_pool = keep.tile([P, T], I32, name="word_pool", align_bytes=64)
+        scale_pool = keep.tile([P, T], U8, name="scale_pool", align_bytes=64)
+        bias_pool = keep.tile([P, T], F32, name="bias_pool", align_bytes=64)
+        scale_got = keep.tile([P, N], U8, name="scale_got", align_bytes=64)
+        scale_p1 = keep.tile([P, N], U8, name="scale_p1", align_bytes=64)
+        bias_got = keep.tile([P, N], F32, name="bias_got", align_bytes=64)
+        bias_col = keep.tile([P, N // P], F32, name="bias_col")
+        ident = keep.tile([P, P], F32, name="ident", align_bytes=64)
+        weight = keep.tile([P, 1], F32, name="weight")
+        best = keep.tile([P, N // SEG], F32, name="best")
+        result = keep.tile([P, N // SEG], F32, name="result")
+
+        nc.vector.memset(scale_pool[:].bitcast(I32), 0)
+        nc.vector.memset(bias_pool[0 : P - 1, :], 0.0)
+        nc.gpsimd.memset(scale_p1[:].bitcast(I32), 0)
+        make_identity(nc, ident[:])
+
+        nc.sync.dma_start(offsets[:], offs)
+        nc.sync.dma_start(out=bias_pool[P - 1 : P, :], in_=kb[0:1, :])
+        nc.sync.dma_start(out=word_pool[:], in_=k_words[0].rearrange("p t b -> p (t b)").bitcast(I32))
+        for quad in range(4):
+            nc.scalar.dma_start(
+                out=scale_pool[32 * quad : 32 * quad + 8, :].bitcast(I32),
+                in_=k_scales[:, 4 * quad : 4 * quad + 4, :].bitcast(I32),
+            )
+        q_raw = []
+        for g in range(PASSES):
+            raw = keep.tile([P, 4, NQ], F32, name="q_raw%d" % g)
+            nc.sync.dma_start(out=raw[:], in_=qT[0, g * KP : (g + 1) * KP, :].rearrange("(p j) w -> p j w", j=4))
+            q_raw.append(raw)
+        nc.sync.dma_start(out=weight[:], in_=pw[0])
+
+        nc.vector.tensor_copy(bias_got[:], bias_pool[:].indirect(offsets[:]))
+        nc.vector.tensor_copy(scale_got[:], scale_pool[:].indirect(offsets[:]))
+
+        for h in range(2):
+            turned = psum.tile([P, 4, P], F32, name="turned%d" % h)
+            for b in range(4):
+                c0 = h * HALF + b * P
+                nc.tensor.transpose(turned[:, b, :], bias_got[:, c0 : c0 + P], ident[:])
+            nc.scalar.copy(bias_col[:, 4 * h : 4 * h + 4], turned[:, :, P - 1])
+        for quad in range(4):
+            nc.scalar.dma_start(
+                out=scale_p1[32 * quad : 32 * quad + 4, :].bitcast(I32),
+                in_=scale_got[32 * quad + 4 : 32 * quad + 8, :].bitcast(I32),
+            )
+        spread = []
+        for h in range(2):
+            bank = psum.tile([P, 4, P], F32, name="spread%d" % h)
+            for b in range(4):
+                m = 4 * h + b
+                nc.tensor.transpose(bank[:, b, :], bias_col[:, m : m + 1].to_broadcast([P, P]), ident[:])
+            spread.append(bank)
+
+        q_bf = []
+        for g in range(PASSES):
+            grouped = keep.tile([P, NQ, 4], BF16, name="q_bf%d" % g, align_bytes=64)
+            nc.scalar.copy(grouped[:], q_raw[g][:].rearrange("p j w -> p w j"))
+            q_bf.append(grouped)
+        bias_rows = []
+        for h in range(2):
+            rows = keep.tile([P, HALF], F32, name="bias_rows%d" % h)
+            nc.scalar.copy(rows[:], spread[h][:].rearrange("p b n -> p (b n)"))
+            bias_rows.append(rows)
+
+        got = [keep.tile([P, HALF], U32, name="word_got%d" % h, align_bytes=64) for h in range(2)]
+        parted = [keep.tile([P, PASSES, 2 * HALF], U8, name="parted%d" % h, align_bytes=64) for h in range(2)]
+        q_codes = [keep.tile([P, NQ], U32, name="q_codes%d" % g, align_bytes=64) for g in range(PASSES)]
+        q_scales = [keep.tile([P, NQ], U8, name="q_scales%d" % g, align_bytes=64) for g in range(PASSES)]
+
+        def gather_words(h):
+            cols = HALF // 16
+            nc.vector.tensor_copy(got[h][:], word_pool[:].bitcast(U32).indirect(offsets[:, h * cols : (h + 1) * cols]))
+
+        def part_words(h):
+            nc.vector.tensor_copy(
+                parted[h][:].bitcast(U16), got[h][:].bitcast(U16).rearrange("p (n g) -> p g n", g=PASSES)
+            )
+
+        def quantise(g):
+            nc.vector.quantize_mx(
+                out=q_codes[g][:].bitcast(FP8X4), scales=q_scales[g][:], in_=q_bf[g][:].rearrange("p w j -> p (w j)")
+            )
+
+        gather_words(0)
+        gather_words(1)
+        part_words(0)
+        quantise(0)
+        quantise(1)
+        part_words(1)
+
+        planes = [scale_got, scale_p1]
+        sums = []
+        for h in range(2):
+            scores = psum.tile([P, HALF], F32, name="scores%d" % h)
+            for g in range(PASSES):
+                nc.tensor.matmul_mx(
+                    out=scores[:],
+                    lhsT=q_codes[g][:].bitcast(FP8X4),
+                    lhsT_scale=q_scales[g][:],
+                    rhs=parted[h][:, g, :].bitcast(FP4X4),
+                    rhs_scale=planes[g][:, h * HALF : (h + 1) * HALF],
+                    start=(g == 0),
+                    stop=(g == PASSES - 1),
+                )
+            total = keep.tile([P, HALF], F32, name="total%d" % h)
+            nc.vector.tensor_tensor(total[:], scores[:], bias_rows[h][:], add)
+            sums.append(total)
+        pages = HALF // SEG
+        for h in range(2):
+            nc.vector.tensor_reduce(
+                best[:, h * pages : (h + 1) * pages],
+                sums[h][:].rearrange("p (j s) -> p j s", s=SEG),
+                mybir.AxisListType.X,
+                amax,
+            )
+        nc.vector.tensor_scalar_mul(result[:], best[:], weight[:])
+        nc.sync.dma_start(out=out[0], in_=result[:])

@@ -18,8 +18,11 @@ N = 1024
 NQ = 128
 SEG = 32
 HALF = 512
+UNIT = 256
+UNITS = N // UNIT
 PASSES = 2
 KP = 512
+ROWS0 = 96
 
 FLOPS = 2 * 1024 * N * NQ
 BYTES = P * T * 4 + 32 * T + 1024 * NQ * 4 + T * 4 + NQ * 4 + P * 64 * 2 + NQ * 32 * 4
@@ -35,120 +38,119 @@ def tile_attend_page_prior_kernel(tc, qT, k_words, k_scales, kb, pw, offs, out):
 
         offsets = keep.tile([P, N // 16], U16, name="offsets")
         word_pool = keep.tile([P, T], I32, name="word_pool", align_bytes=64)
-        scale_pool = keep.tile([P, T], U8, name="scale_pool", align_bytes=64)
+        scale_pool = keep.tile([P, T + 4], U8, name="scale_pool", align_bytes=64)
         bias_pool = keep.tile([P, T], F32, name="bias_pool", align_bytes=64)
         scale_got = keep.tile([P, N], U8, name="scale_got", align_bytes=64)
-        scale_p1 = keep.tile([P, N], U8, name="scale_p1", align_bytes=64)
-        bias_got = keep.tile([P, N], F32, name="bias_got", align_bytes=64)
+        planes = keep.tile([P, PASSES * N + 4], U8, name="planes", align_bytes=64)
         bias_col = keep.tile([P, N // P], F32, name="bias_col")
+        ident_made = keep.tile([P, P], F32, name="ident_made", align_bytes=64)
         ident = keep.tile([P, P], F32, name="ident", align_bytes=64)
         weight = keep.tile([P, 1], F32, name="weight")
         best = keep.tile([P, N // SEG], F32, name="best")
         result = keep.tile([P, N // SEG], F32, name="result")
-
-        nc.vector.memset(scale_pool[:].bitcast(I32), 0)
-        nc.vector.memset(bias_pool[0 : P - 1, :], 0.0)
-        nc.gpsimd.memset(scale_p1[:].bitcast(I32), 0)
-        make_identity(nc, ident[:])
+        q_raw = keep.tile([P, PASSES, 4, NQ], F32, name="q_raw")
 
         nc.sync.dma_start(offsets[:], offs)
+        nc.sync.dma_start(
+            out=scale_pool[ROWS0:P, 0:T].bitcast(I32), in_=k_scales.rearrange("o f t -> (o f) t").bitcast(I32)
+        )
         nc.sync.dma_start(out=bias_pool[P - 1 : P, :], in_=kb[0:1, :])
+        nc.scalar.dma_start(out=weight[:], in_=pw[0])
+        nc.sync.dma_start(out=q_raw[:], in_=qT[0].rearrange("(g p j) w -> p g j w", g=PASSES, j=4))
         nc.sync.dma_start(out=word_pool[:], in_=k_words[0].rearrange("p t b -> p (t b)").bitcast(I32))
-        for quad in range(4):
-            nc.scalar.dma_start(
-                out=scale_pool[32 * quad : 32 * quad + 8, :].bitcast(I32),
-                in_=k_scales[:, 4 * quad : 4 * quad + 4, :].bitcast(I32),
-            )
-        q_raw = []
-        for g in range(PASSES):
-            raw = keep.tile([P, 4, NQ], F32, name="q_raw%d" % g)
-            nc.sync.dma_start(out=raw[:], in_=qT[0, g * KP : (g + 1) * KP, :].rearrange("(p j) w -> p j w", j=4))
-            q_raw.append(raw)
-        nc.sync.dma_start(out=weight[:], in_=pw[0])
 
-        nc.vector.tensor_copy(bias_got[:], bias_pool[:].indirect(offsets[:]))
-        nc.vector.tensor_copy(scale_got[:], scale_pool[:].indirect(offsets[:]))
-
-        for h in range(2):
-            turned = psum.tile([P, 4, P], F32, name="turned%d" % h)
-            for b in range(4):
-                c0 = h * HALF + b * P
-                nc.tensor.transpose(turned[:, b, :], bias_got[:, c0 : c0 + P], ident[:])
-            nc.scalar.copy(bias_col[:, 4 * h : 4 * h + 4], turned[:, :, P - 1])
-        for quad in range(4):
-            nc.scalar.dma_start(
-                out=scale_p1[32 * quad : 32 * quad + 4, :].bitcast(I32),
-                in_=scale_got[32 * quad + 4 : 32 * quad + 8, :].bitcast(I32),
-            )
-        spread = []
-        for h in range(2):
-            bank = psum.tile([P, 4, P], F32, name="spread%d" % h)
-            for b in range(4):
-                m = 4 * h + b
-                nc.tensor.transpose(bank[:, b, :], bias_col[:, m : m + 1].to_broadcast([P, P]), ident[:])
-            spread.append(bank)
+        make_identity(nc, ident_made[:])
+        nc.gpsimd.memset(bias_pool[0 : P - 1, :], 0.0)
+        nc.vector.memset(scale_pool[0:ROWS0, :].bitcast(I32), 0)
+        nc.vector.memset(planes[:].bitcast(I32), 0)
+        nc.scalar.copy(ident[:], ident_made[:])
 
         q_bf = []
         for g in range(PASSES):
             grouped = keep.tile([P, NQ, 4], BF16, name="q_bf%d" % g, align_bytes=64)
-            nc.scalar.copy(grouped[:], q_raw[g][:].rearrange("p j w -> p w j"))
+            nc.scalar.copy(grouped[:], q_raw[:, g, :, :].rearrange("p j w -> p w j"))
             q_bf.append(grouped)
-        bias_rows = []
-        for h in range(2):
-            rows = keep.tile([P, HALF], F32, name="bias_rows%d" % h)
-            nc.scalar.copy(rows[:], spread[h][:].rearrange("p b n -> p (b n)"))
-            bias_rows.append(rows)
 
-        got = [keep.tile([P, HALF], U32, name="word_got%d" % h, align_bytes=64) for h in range(2)]
-        parted = [keep.tile([P, PASSES, 2 * HALF], U8, name="parted%d" % h, align_bytes=64) for h in range(2)]
+        nc.vector.tensor_copy(scale_got[:], scale_pool[:, 0:T].indirect(offsets[:]))
+        for g in range(PASSES):
+            for quad in range(4):
+                row = ROWS0 + 16 * g + 4 * quad
+                nc.sync.dma_start(
+                    out=planes[32 * quad : 32 * quad + 4, g * N : (g + 1) * N].bitcast(I32),
+                    in_=scale_got[row : row + 4, :].bitcast(I32),
+                )
+
         q_codes = [keep.tile([P, NQ], U32, name="q_codes%d" % g, align_bytes=64) for g in range(PASSES)]
         q_scales = [keep.tile([P, NQ], U8, name="q_scales%d" % g, align_bytes=64) for g in range(PASSES)]
-
-        def gather_words(h):
-            cols = HALF // 16
-            nc.vector.tensor_copy(got[h][:], word_pool[:].bitcast(U32).indirect(offsets[:, h * cols : (h + 1) * cols]))
-
-        def part_words(h):
-            nc.vector.tensor_copy(
-                parted[h][:].bitcast(U16), got[h][:].bitcast(U16).rearrange("p (n g) -> p g n", g=PASSES)
-            )
-
-        def quantise(g):
+        for g in range(PASSES):
             nc.vector.quantize_mx(
                 out=q_codes[g][:].bitcast(FP8X4), scales=q_scales[g][:], in_=q_bf[g][:].rearrange("p w j -> p (w j)")
             )
 
-        gather_words(0)
-        gather_words(1)
-        part_words(0)
-        quantise(0)
-        quantise(1)
-        part_words(1)
+        cols = HALF // 16
+        for h in range(2):
+            bias_got = keep.tile([P, HALF], F32, name="bias_got%d" % h, align_bytes=64)
+            nc.vector.tensor_copy(bias_got[:], bias_pool[:].indirect(offsets[:, h * cols : (h + 1) * cols]))
+            turned = psum.tile([P, 4, P], F32, name="turned%d" % h)
+            for b in range(4):
+                nc.tensor.transpose(turned[:, b, :], bias_got[:, b * P : (b + 1) * P], ident[:])
+            nc.scalar.copy(bias_col[:, 4 * h : 4 * h + 4], turned[:, :, P - 1])
+        bias_rows = []
+        for h in range(2):
+            spread = psum.tile([P, 4, P], F32, name="spread%d" % h)
+            for b in range(4):
+                m = 4 * h + b
+                nc.tensor.transpose(spread[:, b, :], bias_col[:, m : m + 1].to_broadcast([P, P]), ident[:])
+            rows = keep.tile([P, HALF], F32, name="bias_rows%d" % h)
+            nc.scalar.copy(rows[:], spread[:].rearrange("p b n -> p (b n)"))
+            bias_rows.append(rows)
 
-        planes = [scale_got, scale_p1]
-        sums = []
+        got = [keep.tile([P, HALF], U32, name="word_got%d" % h, align_bytes=64) for h in range(2)]
         for h in range(2):
-            scores = psum.tile([P, HALF], F32, name="scores%d" % h)
-            for g in range(PASSES):
-                nc.tensor.matmul_mx(
-                    out=scores[:],
-                    lhsT=q_codes[g][:].bitcast(FP8X4),
-                    lhsT_scale=q_scales[g][:],
-                    rhs=parted[h][:, g, :].bitcast(FP4X4),
-                    rhs_scale=planes[g][:, h * HALF : (h + 1) * HALF],
-                    start=(g == 0),
-                    stop=(g == PASSES - 1),
-                )
-            total = keep.tile([P, HALF], F32, name="total%d" % h)
-            nc.vector.tensor_tensor(total[:], scores[:], bias_rows[h][:], add)
-            sums.append(total)
-        pages = HALF // SEG
-        for h in range(2):
+            nc.vector.tensor_copy(got[h][:], word_pool[:].bitcast(U32).indirect(offsets[:, h * cols : (h + 1) * cols]))
+
+        scores = []
+        for u in range(UNITS):
+            parted = keep.tile([P, PASSES, 2 * UNIT], U8, name="parted%d" % u, align_bytes=64)
+            c0 = (u % 2) * UNIT
+            nc.vector.tensor_copy(
+                parted[:].bitcast(U16),
+                got[u // 2][:, c0 : c0 + UNIT].bitcast(U16).rearrange("p (n g) -> p g n", g=PASSES),
+            )
+            bank = psum.tile([P, UNIT], F32, name="scores%d" % u)
+            for b in range(UNIT // P):
+                s0 = u * UNIT + b * P
+                for g in range(PASSES):
+                    nc.tensor.matmul_mx(
+                        out=bank[:, b * P : (b + 1) * P],
+                        lhsT=q_codes[g][:].bitcast(FP8X4),
+                        lhsT_scale=q_scales[g][:],
+                        rhs=parted[:, g, 2 * P * b : 2 * P * (b + 1)].bitcast(FP4X4),
+                        rhs_scale=planes[:, g * N + s0 : g * N + s0 + P],
+                        start=(g == 0),
+                        stop=(g == PASSES - 1),
+                    )
+            scores.append(bank)
+
+        totals = [keep.tile([P, UNIT], F32, name="total%d" % u) for u in range(UNITS)]
+        pages = UNIT // SEG
+
+        def add_bias(u):
+            c0 = (u % 2) * UNIT
+            nc.vector.tensor_tensor(totals[u][:], scores[u][:], bias_rows[u // 2][:, c0 : c0 + UNIT], add)
+
+        def page_max(u):
             nc.vector.tensor_reduce(
-                best[:, h * pages : (h + 1) * pages],
-                sums[h][:].rearrange("p (j s) -> p j s", s=SEG),
+                best[:, u * pages : (u + 1) * pages],
+                totals[u][:].rearrange("p (j s) -> p j s", s=SEG),
                 mybir.AxisListType.X,
                 amax,
             )
+
+        add_bias(0)
+        for u in range(1, UNITS):
+            add_bias(u)
+            page_max(u - 1)
+        page_max(UNITS - 1)
         nc.vector.tensor_scalar_mul(result[:], best[:], weight[:])
         nc.sync.dma_start(out=out[0], in_=result[:])

@@ -22,7 +22,7 @@ UNIT = 256
 UNITS = N // UNIT
 PASSES = 2
 KP = 512
-ROWS0 = 96
+ROWS = 32
 
 FLOPS = 2 * 1024 * N * NQ
 BYTES = P * T * 4 + 32 * T + 1024 * NQ * 4 + T * 4 + NQ * 4 + P * 64 * 2 + NQ * 32 * 4
@@ -41,28 +41,27 @@ def tile_attend_page_prior_kernel(tc, qT, k_words, k_scales, kb, pw, offs, out):
         scale_pool = keep.tile([P, T + 4], U8, name="scale_pool", align_bytes=64)
         bias_pool = keep.tile([P, T], F32, name="bias_pool", align_bytes=64)
         scale_got = keep.tile([P, N], U8, name="scale_got", align_bytes=64)
-        planes = keep.tile([P, PASSES * N + 4], U8, name="planes", align_bytes=64)
-        bias_col = keep.tile([P, N // P], F32, name="bias_col")
+        planes = [keep.tile([P, N + 4], U8, name="plane%d" % g, align_bytes=64) for g in range(PASSES)]
+        bias_col = keep.tile([P, N // P], F32, name="bias_col", tag="column")
         ident_made = keep.tile([P, P], F32, name="ident_made", align_bytes=64)
         ident = keep.tile([P, P], F32, name="ident", align_bytes=64)
-        weight = keep.tile([P, 1], F32, name="weight")
         best = keep.tile([P, N // SEG], F32, name="best")
         result = keep.tile([P, N // SEG], F32, name="result")
         q_raw = keep.tile([P, PASSES, 4, NQ], F32, name="q_raw")
 
         nc.sync.dma_start(offsets[:], offs)
         nc.sync.dma_start(
-            out=scale_pool[ROWS0:P, 0:T].bitcast(I32), in_=k_scales.rearrange("o f t -> (o f) t").bitcast(I32)
+            out=scale_pool[0:ROWS, 0:T].bitcast(I32), in_=k_scales.rearrange("o f t -> (o f) t").bitcast(I32)
         )
-        nc.sync.dma_start(out=bias_pool[P - 1 : P, :], in_=kb[0:1, :])
-        nc.scalar.dma_start(out=weight[:], in_=pw[0])
+        nc.scalar.dma_start(out=bias_pool[P - 1 : P, :], in_=kb[0:1, :])
         nc.sync.dma_start(out=q_raw[:], in_=qT[0].rearrange("(g p j) w -> p g j w", g=PASSES, j=4))
         nc.sync.dma_start(out=word_pool[:], in_=k_words[0].rearrange("p t b -> p (t b)").bitcast(I32))
 
         make_identity(nc, ident_made[:])
         nc.gpsimd.memset(bias_pool[0 : P - 1, :], 0.0)
-        nc.vector.memset(scale_pool[0:ROWS0, :].bitcast(I32), 0)
-        nc.vector.memset(planes[:].bitcast(I32), 0)
+        nc.vector.memset(scale_pool[32:64, :].bitcast(I32), 0)
+        nc.vector.memset(scale_pool[64:P, :].bitcast(I32), 0)
+        nc.vector.memset(planes[1][:].bitcast(I32), 0)
         nc.scalar.copy(ident[:], ident_made[:])
 
         q_bf = []
@@ -72,13 +71,13 @@ def tile_attend_page_prior_kernel(tc, qT, k_words, k_scales, kb, pw, offs, out):
             q_bf.append(grouped)
 
         nc.vector.tensor_copy(scale_got[:], scale_pool[:, 0:T].indirect(offsets[:]))
-        for g in range(PASSES):
-            for quad in range(4):
-                row = ROWS0 + 16 * g + 4 * quad
-                nc.sync.dma_start(
-                    out=planes[32 * quad : 32 * quad + 4, g * N : (g + 1) * N].bitcast(I32),
-                    in_=scale_got[row : row + 4, :].bitcast(I32),
-                )
+        nc.vector.tensor_copy(planes[0][:, 0:N].bitcast(I32), scale_got[:].bitcast(I32))
+        for g, quad in [(1, 0), (1, 1), (1, 2), (1, 3), (0, 1), (0, 2), (0, 3)]:
+            row = 16 * g + 4 * quad
+            nc.sync.dma_start(
+                out=planes[g][32 * quad : 32 * quad + 4, 0:N].bitcast(I32),
+                in_=scale_got[row : row + 4, :].bitcast(I32),
+            )
 
         q_codes = [keep.tile([P, NQ], U32, name="q_codes%d" % g, align_bytes=64) for g in range(PASSES)]
         q_scales = [keep.tile([P, NQ], U8, name="q_scales%d" % g, align_bytes=64) for g in range(PASSES)]
@@ -105,6 +104,9 @@ def tile_attend_page_prior_kernel(tc, qT, k_words, k_scales, kb, pw, offs, out):
             nc.scalar.copy(rows[:], spread[:].rearrange("p b n -> p (b n)"))
             bias_rows.append(rows)
 
+        weight = keep.tile([P, 1], F32, name="weight", tag="column")
+        nc.sync.dma_start(out=weight[:], in_=pw[0])
+
         got = [keep.tile([P, HALF], U32, name="word_got%d" % h, align_bytes=64) for h in range(2)]
         for h in range(2):
             nc.vector.tensor_copy(got[h][:], word_pool[:].bitcast(U32).indirect(offsets[:, h * cols : (h + 1) * cols]))
@@ -126,7 +128,7 @@ def tile_attend_page_prior_kernel(tc, qT, k_words, k_scales, kb, pw, offs, out):
                         lhsT=q_codes[g][:].bitcast(FP8X4),
                         lhsT_scale=q_scales[g][:],
                         rhs=parted[:, g, 2 * P * b : 2 * P * (b + 1)].bitcast(FP4X4),
-                        rhs_scale=planes[:, g * N + s0 : g * N + s0 + P],
+                        rhs_scale=planes[g][:, s0 : s0 + P],
                         start=(g == 0),
                         stop=(g == PASSES - 1),
                     )

@@ -37,122 +37,138 @@ def tile_attend_page_prior_kernel(tc, qT, k_words, k_scales, kb, pw, offs, out):
         psum = ctx.enter_context(tc.psum_pool(name="psum", bufs=1))
 
         offsets = keep.tile([P, N // 16], U16, name="offsets")
-        word_pool = keep.tile([P, T], I32, name="word_pool", align_bytes=64)
+        word_pool = keep.tile([P, T], I32, name="word_pool", tag="words", align_bytes=64)
         scale_pool = keep.tile([P, T + 4], U8, name="scale_pool", align_bytes=64)
-        bias_pool = keep.tile([P, T], F32, name="bias_pool", align_bytes=64)
+        bias_pool = keep.tile([P, T], F32, name="bias_pool", tag="wide", align_bytes=64)
         scale_got = keep.tile([P, N], U8, name="scale_got", align_bytes=64)
         planes = [keep.tile([P, N + 4], U8, name="plane%d" % g, align_bytes=64) for g in range(PASSES)]
         bias_col = keep.tile([P, N // P], F32, name="bias_col", tag="column")
-        ident_made = keep.tile([P, P], F32, name="ident_made", align_bytes=64)
         ident = keep.tile([P, P], F32, name="ident", align_bytes=64)
         best = keep.tile([P, N // SEG], F32, name="best")
         result = keep.tile([P, N // SEG], F32, name="result")
-        q_raw = keep.tile([P, PASSES, 4, NQ], F32, name="q_raw")
+        q_raw = [keep.tile([P, 4, NQ], F32, name="q_raw%d" % g, tag="raw%d" % g, align_bytes=64) for g in range(PASSES)]
 
         nc.sync.dma_start(offsets[:], offs)
         nc.sync.dma_start(
             out=scale_pool[0:ROWS, 0:T].bitcast(I32), in_=k_scales.rearrange("o f t -> (o f) t").bitcast(I32)
         )
         nc.scalar.dma_start(out=bias_pool[P - 1 : P, :], in_=kb[0:1, :])
-        nc.sync.dma_start(out=q_raw[:], in_=qT[0].rearrange("(g p j) w -> p g j w", g=PASSES, j=4))
         nc.sync.dma_start(out=word_pool[:], in_=k_words[0].rearrange("p t b -> p (t b)").bitcast(I32))
+        for g in range(PASSES):
+            nc.sync.dma_start(out=q_raw[g][:], in_=qT[0, g * KP : (g + 1) * KP, :].rearrange("(p j) w -> p j w", j=4))
 
-        make_identity(nc, ident_made[:])
         nc.gpsimd.memset(bias_pool[0 : P - 1, :], 0.0)
+        make_identity(nc, ident[:])
         nc.vector.memset(scale_pool[32:64, :].bitcast(I32), 0)
         nc.vector.memset(scale_pool[64:P, :].bitcast(I32), 0)
         nc.vector.memset(planes[1][:].bitcast(I32), 0)
-        nc.scalar.copy(ident[:], ident_made[:])
-
-        q_bf = []
-        for g in range(PASSES):
-            grouped = keep.tile([P, NQ, 4], BF16, name="q_bf%d" % g, align_bytes=64)
-            nc.scalar.copy(grouped[:], q_raw[:, g, :, :].rearrange("p j w -> p w j"))
-            q_bf.append(grouped)
 
         nc.vector.tensor_copy(scale_got[:], scale_pool[:, 0:T].indirect(offsets[:]))
         nc.vector.tensor_copy(planes[0][:, 0:N].bitcast(I32), scale_got[:].bitcast(I32))
-        for g, quad in [(1, 0), (1, 1), (1, 2), (1, 3), (0, 1), (0, 2), (0, 3)]:
+        for g, quad in [(0, 1), (0, 2), (0, 3), (1, 0), (1, 1), (1, 2), (1, 3)]:
             row = 16 * g + 4 * quad
             nc.sync.dma_start(
                 out=planes[g][32 * quad : 32 * quad + 4, 0:N].bitcast(I32),
                 in_=scale_got[row : row + 4, :].bitcast(I32),
             )
 
-        q_codes = [keep.tile([P, NQ], U32, name="q_codes%d" % g, align_bytes=64) for g in range(PASSES)]
-        q_scales = [keep.tile([P, NQ], U8, name="q_scales%d" % g, align_bytes=64) for g in range(PASSES)]
-        for g in range(PASSES):
-            nc.vector.quantize_mx(
-                out=q_codes[g][:].bitcast(FP8X4), scales=q_scales[g][:], in_=q_bf[g][:].rearrange("p w j -> p (w j)")
-            )
-
         cols = HALF // 16
         for h in range(2):
-            bias_got = keep.tile([P, HALF], F32, name="bias_got%d" % h, align_bytes=64)
+            bias_got = keep.tile([P, HALF], F32, name="bias_got%d" % h, tag="half%d" % h, align_bytes=64)
             nc.vector.tensor_copy(bias_got[:], bias_pool[:].indirect(offsets[:, h * cols : (h + 1) * cols]))
             turned = psum.tile([P, 4, P], F32, name="turned%d" % h)
             for b in range(4):
                 nc.tensor.transpose(turned[:, b, :], bias_got[:, b * P : (b + 1) * P], ident[:])
             nc.scalar.copy(bias_col[:, 4 * h : 4 * h + 4], turned[:, :, P - 1])
-        bias_rows = []
+        spread = []
         for h in range(2):
-            spread = psum.tile([P, 4, P], F32, name="spread%d" % h)
+            bank = psum.tile([P, 4, P], F32, name="spread%d" % h)
             for b in range(4):
                 m = 4 * h + b
-                nc.tensor.transpose(spread[:, b, :], bias_col[:, m : m + 1].to_broadcast([P, P]), ident[:])
-            rows = keep.tile([P, HALF], F32, name="bias_rows%d" % h)
-            nc.scalar.copy(rows[:], spread[:].rearrange("p b n -> p (b n)"))
-            bias_rows.append(rows)
+                nc.tensor.transpose(bank[:, b, :], bias_col[:, m : m + 1].to_broadcast([P, P]), ident[:])
+            spread.append(bank)
 
         weight = keep.tile([P, 1], F32, name="weight", tag="column")
         nc.sync.dma_start(out=weight[:], in_=pw[0])
 
-        got = [keep.tile([P, HALF], U32, name="word_got%d" % h, align_bytes=64) for h in range(2)]
+        q_bf = []
+        for g in range(PASSES):
+            grouped = keep.tile([P, NQ, 4], BF16, name="q_bf%d" % g, tag="half%d" % (1 - g), align_bytes=64)
+            nc.scalar.copy(grouped[:], q_raw[g][:].rearrange("p j w -> p w j"))
+            q_bf.append(grouped)
+        bias_rows = []
         for h in range(2):
-            nc.vector.tensor_copy(got[h][:], word_pool[:].bitcast(U32).indirect(offsets[:, h * cols : (h + 1) * cols]))
+            rows = keep.tile([P, HALF], F32, name="bias_rows%d" % h)
+            nc.scalar.copy(rows[:], spread[h][:].rearrange("p b n -> p (b n)"))
+            bias_rows.append(rows)
 
+        got = keep.tile([P, N], U32, name="word_got", tag="wide", align_bytes=64)
+        for h in range(2):
+            nc.vector.tensor_copy(
+                got[:, h * HALF : (h + 1) * HALF],
+                word_pool[:].bitcast(U32).indirect(offsets[:, h * cols : (h + 1) * cols]),
+            )
+
+        codes = keep.tile([P, PASSES * NQ], U32, name="codes", tag="words", align_bytes=64)
+        q_codes = [codes[:, g * NQ : (g + 1) * NQ] for g in range(PASSES)]
+        q_scales = [keep.tile([P, NQ], U8, name="q_scales%d" % g, align_bytes=64) for g in range(PASSES)]
+        parted_first = keep.tile([P, PASSES * 2 * UNIT], U8, name="parted_first", align_bytes=64)
+        parted_rest = keep.tile([P, (UNITS - 1) * PASSES * 2 * UNIT], U8, name="parted_rest", tag="raw1", align_bytes=64)
+        width = PASSES * 2 * UNIT
+        parted = [parted_first[:]] + [parted_rest[:, u * width : (u + 1) * width] for u in range(UNITS - 1)]
+
+        def part(u):
+            nc.vector.tensor_copy(
+                parted[u].bitcast(U16).rearrange("p (g n) -> p g n", g=PASSES),
+                got[:, u * UNIT : (u + 1) * UNIT].bitcast(U16).rearrange("p (n g) -> p g n", g=PASSES),
+            )
+
+        part(0)
+        for g in range(PASSES):
+            nc.vector.quantize_mx(
+                out=q_codes[g].bitcast(FP8X4), scales=q_scales[g][:], in_=q_bf[g][:].rearrange("p w j -> p (w j)")
+            )
         scores = []
         for u in range(UNITS):
-            parted = keep.tile([P, PASSES, 2 * UNIT], U8, name="parted%d" % u, align_bytes=64)
-            c0 = (u % 2) * UNIT
-            nc.vector.tensor_copy(
-                parted[:].bitcast(U16),
-                got[u // 2][:, c0 : c0 + UNIT].bitcast(U16).rearrange("p (n g) -> p g n", g=PASSES),
-            )
+            if u > 0:
+                part(u)
             bank = psum.tile([P, UNIT], F32, name="scores%d" % u)
             for b in range(UNIT // P):
                 s0 = u * UNIT + b * P
                 for g in range(PASSES):
+                    c0 = g * 2 * UNIT + 2 * P * b
                     nc.tensor.matmul_mx(
                         out=bank[:, b * P : (b + 1) * P],
-                        lhsT=q_codes[g][:].bitcast(FP8X4),
+                        lhsT=q_codes[g].bitcast(FP8X4),
                         lhsT_scale=q_scales[g][:],
-                        rhs=parted[:, g, 2 * P * b : 2 * P * (b + 1)].bitcast(FP4X4),
+                        rhs=parted[u][:, c0 : c0 + 2 * P].bitcast(FP4X4),
                         rhs_scale=planes[g][:, s0 : s0 + P],
                         start=(g == 0),
                         stop=(g == PASSES - 1),
                     )
             scores.append(bank)
 
-        totals = [keep.tile([P, UNIT], F32, name="total%d" % u) for u in range(UNITS)]
-        pages = UNIT // SEG
+        spans = [(u * UNIT, UNIT) for u in range(UNITS)]
+        totals = [keep.tile([P, w], F32, name="total%d" % u) for u, (s0, w) in enumerate(spans)]
 
         def add_bias(u):
-            c0 = (u % 2) * UNIT
-            nc.vector.tensor_tensor(totals[u][:], scores[u][:], bias_rows[u // 2][:, c0 : c0 + UNIT], add)
+            s0, w = spans[u]
+            c0 = s0 % HALF
+            nc.vector.tensor_tensor(totals[u][:], scores[u][:], bias_rows[s0 // HALF][:, c0 : c0 + w], add)
 
         def page_max(u):
+            s0, w = spans[u]
             nc.vector.tensor_reduce(
-                best[:, u * pages : (u + 1) * pages],
+                best[:, s0 // SEG : (s0 + w) // SEG],
                 totals[u][:].rearrange("p (j s) -> p j s", s=SEG),
                 mybir.AxisListType.X,
                 amax,
             )
 
         add_bias(0)
-        for u in range(1, UNITS):
+        for u in range(1, len(spans)):
             add_bias(u)
             page_max(u - 1)
-        page_max(UNITS - 1)
+        page_max(len(spans) - 1)
         nc.vector.tensor_scalar_mul(result[:], best[:], weight[:])
         nc.sync.dma_start(out=out[0], in_=result[:])

@@ -39,10 +39,10 @@ def tile_attend_page_prior_kernel(tc, qT, k_words, k_scales, kb, pw, offs, out):
         offsets = keep.tile([P, N // 16], U16, name="offsets")
         word_pool = keep.tile([P, T], I32, name="word_pool", tag="words", align_bytes=64)
         scale_pool = keep.tile([P, T + 4], U8, name="scale_pool", align_bytes=64)
-        bias_pool = keep.tile([P, T], F32, name="bias_pool", tag="wide", align_bytes=64)
+        bias_pool = keep.tile([P, T], F32, name="bias_pool", align_bytes=64)
         scale_got = keep.tile([P, N], U8, name="scale_got", align_bytes=64)
-        planes = [keep.tile([P, N + 4], U8, name="plane%d" % g, align_bytes=64) for g in range(PASSES)]
-        bias_col = keep.tile([P, N // P], F32, name="bias_col", tag="column")
+        planes = keep.tile([P, PASSES * N], U8, name="planes", align_bytes=64)
+        bias_col = [keep.tile([P, HALF // P], F32, name="bias_col%d" % h, tag="column%d" % h) for h in range(2)]
         ident = keep.tile([P, P], F32, name="ident", align_bytes=64)
         best = keep.tile([P, N // SEG], F32, name="best")
         result = keep.tile([P, N // SEG], F32, name="result")
@@ -50,72 +50,74 @@ def tile_attend_page_prior_kernel(tc, qT, k_words, k_scales, kb, pw, offs, out):
 
         nc.sync.dma_start(offsets[:], offs)
         nc.sync.dma_start(
-            out=scale_pool[0:ROWS, 0:T].bitcast(I32), in_=k_scales.rearrange("o f t -> (o f) t").bitcast(I32)
+            out=scale_pool[0:ROWS, 0:T].bitcast(I32), in_=k_scales.bitcast(I32).rearrange("o f t -> f o t")
         )
         nc.scalar.dma_start(out=bias_pool[P - 1 : P, :], in_=kb[0:1, :])
+        q_rows = qT[0].rearrange("(g p j) w -> g p j w", g=PASSES, j=4)
+        nc.sync.dma_start(out=q_raw[0][:], in_=q_rows[0])
         nc.sync.dma_start(out=word_pool[:], in_=k_words[0].rearrange("p t b -> p (t b)").bitcast(I32))
-        for g in range(PASSES):
-            nc.sync.dma_start(out=q_raw[g][:], in_=qT[0, g * KP : (g + 1) * KP, :].rearrange("(p j) w -> p j w", j=4))
+        nc.sync.dma_start(out=q_raw[1][:], in_=q_rows[1])
 
         nc.gpsimd.memset(bias_pool[0 : P - 1, :], 0.0)
         make_identity(nc, ident[:])
+        nc.gpsimd.memset(planes[:].bitcast(I32), 0)
         nc.vector.memset(scale_pool[32:64, :].bitcast(I32), 0)
         nc.vector.memset(scale_pool[64:P, :].bitcast(I32), 0)
-        nc.vector.memset(planes[1][:].bitcast(I32), 0)
 
         nc.vector.tensor_copy(scale_got[:], scale_pool[:, 0:T].indirect(offsets[:]))
-        nc.vector.tensor_copy(planes[0][:, 0:N].bitcast(I32), scale_got[:].bitcast(I32))
-        for g, quad in [(0, 1), (0, 2), (0, 3), (1, 0), (1, 1), (1, 2), (1, 3)]:
-            row = 16 * g + 4 * quad
+        for quad in range(4):
             nc.sync.dma_start(
-                out=planes[g][32 * quad : 32 * quad + 4, 0:N].bitcast(I32),
-                in_=scale_got[row : row + 4, :].bitcast(I32),
+                out=planes[32 * quad : 32 * quad + 4, :].bitcast(I32),
+                in_=scale_got[8 * quad : 8 * quad + 8, :].bitcast(I32),
             )
 
         cols = HALF // 16
+        spread = []
         for h in range(2):
             bias_got = keep.tile([P, HALF], F32, name="bias_got%d" % h, tag="half%d" % h, align_bytes=64)
             nc.vector.tensor_copy(bias_got[:], bias_pool[:].indirect(offsets[:, h * cols : (h + 1) * cols]))
             turned = psum.tile([P, 4, P], F32, name="turned%d" % h)
             for b in range(4):
                 nc.tensor.transpose(turned[:, b, :], bias_got[:, b * P : (b + 1) * P], ident[:])
-            nc.scalar.copy(bias_col[:, 4 * h : 4 * h + 4], turned[:, :, P - 1])
-        spread = []
+            nc.scalar.copy(bias_col[h][:], turned[:, :, P - 1])
         for h in range(2):
             bank = psum.tile([P, 4, P], F32, name="spread%d" % h)
             for b in range(4):
-                m = 4 * h + b
-                nc.tensor.transpose(bank[:, b, :], bias_col[:, m : m + 1].to_broadcast([P, P]), ident[:])
+                nc.tensor.transpose(bank[:, b, :], bias_col[h][:, b : b + 1].to_broadcast([P, P]), ident[:])
             spread.append(bank)
 
-        weight = keep.tile([P, 1], F32, name="weight", tag="column")
+        weight = keep.tile([P, 1], F32, name="weight", tag="column0")
         nc.sync.dma_start(out=weight[:], in_=pw[0])
 
-        q_bf = []
+        q_bf = [
+            keep.tile([P, NQ, 4], BF16, name="q_bf%d" % g, tag=["rounded", "half1"][g], align_bytes=64)
+            for g in range(PASSES)
+        ]
         for g in range(PASSES):
-            grouped = keep.tile([P, NQ, 4], BF16, name="q_bf%d" % g, tag="half%d" % (1 - g), align_bytes=64)
-            nc.scalar.copy(grouped[:], q_raw[g][:].rearrange("p j w -> p w j"))
-            q_bf.append(grouped)
+            nc.scalar.copy(q_bf[g][:], q_raw[g][:].rearrange("p j w -> p w j"))
         bias_rows = []
         for h in range(2):
             rows = keep.tile([P, HALF], F32, name="bias_rows%d" % h)
             nc.scalar.copy(rows[:], spread[h][:].rearrange("p b n -> p (b n)"))
             bias_rows.append(rows)
 
-        got = keep.tile([P, N], U32, name="word_got", tag="wide", align_bytes=64)
-        for h in range(2):
+        got = keep.tile([P, N], U32, name="word_got", tag="half0", align_bytes=64)
+        q_codes = [keep.tile([P, NQ], U32, name="q_codes%d" % g, align_bytes=64) for g in range(PASSES)]
+        q_scales = [keep.tile([P, NQ], U8, name="q_scales%d" % g, align_bytes=64) for g in range(PASSES)]
+        width = PASSES * 2 * UNIT
+        pages = UNIT // SEG
+        scores = {}
+        totals = {}
+
+        def gather_words(h):
             nc.vector.tensor_copy(
                 got[:, h * HALF : (h + 1) * HALF],
                 word_pool[:].bitcast(U32).indirect(offsets[:, h * cols : (h + 1) * cols]),
             )
 
-        codes = keep.tile([P, PASSES * NQ], U32, name="codes", tag="words", align_bytes=64)
-        q_codes = [codes[:, g * NQ : (g + 1) * NQ] for g in range(PASSES)]
-        q_scales = [keep.tile([P, NQ], U8, name="q_scales%d" % g, align_bytes=64) for g in range(PASSES)]
-        parted_first = keep.tile([P, PASSES * 2 * UNIT], U8, name="parted_first", align_bytes=64)
-        parted_rest = keep.tile([P, (UNITS - 1) * PASSES * 2 * UNIT], U8, name="parted_rest", tag="raw1", align_bytes=64)
-        width = PASSES * 2 * UNIT
-        parted = [parted_first[:]] + [parted_rest[:, u * width : (u + 1) * width] for u in range(UNITS - 1)]
+        first = keep.tile([P, width], U8, name="parted_first", align_bytes=64)
+        rest = keep.tile([P, (UNITS - 1) * width], U8, name="parted_rest", tag="raw1", align_bytes=64)
+        parted = [first[:]] + [rest[:, u * width : (u + 1) * width] for u in range(UNITS - 1)]
 
         def part(u):
             nc.vector.tensor_copy(
@@ -123,52 +125,54 @@ def tile_attend_page_prior_kernel(tc, qT, k_words, k_scales, kb, pw, offs, out):
                 got[:, u * UNIT : (u + 1) * UNIT].bitcast(U16).rearrange("p (n g) -> p g n", g=PASSES),
             )
 
-        part(0)
-        for g in range(PASSES):
-            nc.vector.quantize_mx(
-                out=q_codes[g].bitcast(FP8X4), scales=q_scales[g][:], in_=q_bf[g][:].rearrange("p w j -> p (w j)")
-            )
-        scores = []
-        for u in range(UNITS):
-            if u > 0:
-                part(u)
-            bank = psum.tile([P, UNIT], F32, name="scores%d" % u)
+        def score(u):
+            keys = parted[u]
+            scores[u] = psum.tile([P, UNIT], F32, name="scores%d" % u)
             for b in range(UNIT // P):
-                s0 = u * UNIT + b * P
                 for g in range(PASSES):
                     c0 = g * 2 * UNIT + 2 * P * b
+                    s0 = g * N + u * UNIT + b * P
                     nc.tensor.matmul_mx(
-                        out=bank[:, b * P : (b + 1) * P],
-                        lhsT=q_codes[g].bitcast(FP8X4),
+                        out=scores[u][:, b * P : (b + 1) * P],
+                        lhsT=q_codes[g][:].bitcast(FP8X4),
                         lhsT_scale=q_scales[g][:],
-                        rhs=parted[u][:, c0 : c0 + 2 * P].bitcast(FP4X4),
-                        rhs_scale=planes[g][:, s0 : s0 + P],
+                        rhs=keys[:, c0 : c0 + 2 * P].bitcast(FP4X4),
+                        rhs_scale=planes[:, s0 : s0 + P],
                         start=(g == 0),
                         stop=(g == PASSES - 1),
                     )
-            scores.append(bank)
-
-        spans = [(u * UNIT, UNIT) for u in range(UNITS)]
-        totals = [keep.tile([P, w], F32, name="total%d" % u) for u, (s0, w) in enumerate(spans)]
 
         def add_bias(u):
-            s0, w = spans[u]
-            c0 = s0 % HALF
-            nc.vector.tensor_tensor(totals[u][:], scores[u][:], bias_rows[s0 // HALF][:, c0 : c0 + w], add)
+            totals[u] = keep.tile([P, UNIT], F32, name="total%d" % u)
+            c0 = (u % 2) * UNIT
+            nc.vector.tensor_tensor(totals[u][:], scores[u][:], bias_rows[u // 2][:, c0 : c0 + UNIT], add)
 
         def page_max(u):
-            s0, w = spans[u]
             nc.vector.tensor_reduce(
-                best[:, s0 // SEG : (s0 + w) // SEG],
+                best[:, u * pages : (u + 1) * pages],
                 totals[u][:].rearrange("p (j s) -> p j s", s=SEG),
                 mybir.AxisListType.X,
                 amax,
             )
 
+        def quantize(g):
+            nc.vector.quantize_mx(
+                out=q_codes[g][:].bitcast(FP8X4), scales=q_scales[g][:], in_=q_bf[g][:].rearrange("p w j -> p (w j)")
+            )
+
+        quantize(0)
+        gather_words(0)
+        gather_words(1)
+        part(0)
+        quantize(1)
+        for u in range(UNITS):
+            if u > 0:
+                part(u)
+            score(u)
         add_bias(0)
-        for u in range(1, len(spans)):
+        for u in range(1, UNITS):
             add_bias(u)
             page_max(u - 1)
-        page_max(len(spans) - 1)
+        page_max(UNITS - 1)
         nc.vector.tensor_scalar_mul(result[:], best[:], weight[:])
         nc.sync.dma_start(out=out[0], in_=result[:])

@@ -18,8 +18,7 @@ N = 1024
 NQ = 128
 SEG = 32
 HALF = 512
-UNIT = 256
-UNITS = N // UNIT
+WIDTHS = [128, 256, 256, 256, 128]
 PASSES = 2
 KP = 512
 ROWS = 32
@@ -54,9 +53,9 @@ def tile_attend_page_prior_kernel(tc, qT, k_words, k_scales, kb, pw, offs, out):
         )
         nc.scalar.dma_start(out=bias_pool[P - 1 : P, :], in_=kb[0:1, :])
         q_rows = qT[0].rearrange("(g p j) w -> g p j w", g=PASSES, j=4)
-        nc.sync.dma_start(out=q_raw[0][:], in_=q_rows[0])
         nc.sync.dma_start(out=word_pool[:], in_=k_words[0].rearrange("p t b -> p (t b)").bitcast(I32))
-        nc.sync.dma_start(out=q_raw[1][:], in_=q_rows[1])
+        for g in range(PASSES):
+            nc.sync.dma_start(out=q_raw[g][:], in_=q_rows[g])
 
         nc.gpsimd.memset(bias_pool[0 : P - 1, :], 0.0)
         make_identity(nc, ident[:])
@@ -76,7 +75,7 @@ def tile_attend_page_prior_kernel(tc, qT, k_words, k_scales, kb, pw, offs, out):
         for h in range(2):
             bias_got = keep.tile([P, HALF], F32, name="bias_got%d" % h, tag="half%d" % h, align_bytes=64)
             nc.vector.tensor_copy(bias_got[:], bias_pool[:].indirect(offsets[:, h * cols : (h + 1) * cols]))
-            turned = psum.tile([P, 4, P], F32, name="turned%d" % h)
+            turned = psum.tile([P, 4, P], F32, name="turned%d" % h, tag="bank%d" % h)
             for b in range(4):
                 nc.tensor.transpose(turned[:, b, :], bias_got[:, b * P : (b + 1) * P], ident[:])
             nc.scalar.copy(bias_col[h][:], turned[:, :, P - 1])
@@ -89,25 +88,24 @@ def tile_attend_page_prior_kernel(tc, qT, k_words, k_scales, kb, pw, offs, out):
         weight = keep.tile([P, 1], F32, name="weight", tag="column0")
         nc.sync.dma_start(out=weight[:], in_=pw[0])
 
-        q_bf = [
-            keep.tile([P, NQ, 4], BF16, name="q_bf%d" % g, tag=["rounded", "half1"][g], align_bytes=64)
-            for g in range(PASSES)
-        ]
+        q_bf = keep.tile([P, PASSES, NQ, 4], BF16, name="q_bf", tag="half1", align_bytes=64)
         for g in range(PASSES):
-            nc.scalar.copy(q_bf[g][:], q_raw[g][:].rearrange("p j w -> p w j"))
-        bias_rows = []
+            nc.scalar.copy(q_bf[:, g, :, :], q_raw[g][:].rearrange("p j w -> p w j"))
+        bias_rows = keep.tile([P, N], F32, name="bias_rows")
         for h in range(2):
-            rows = keep.tile([P, HALF], F32, name="bias_rows%d" % h)
-            nc.scalar.copy(rows[:], spread[h][:].rearrange("p b n -> p (b n)"))
-            bias_rows.append(rows)
+            nc.scalar.copy(bias_rows[:, h * HALF : (h + 1) * HALF], spread[h][:].rearrange("p b n -> p (b n)"))
 
         got = keep.tile([P, N], U32, name="word_got", tag="half0", align_bytes=64)
-        q_codes = [keep.tile([P, NQ], U32, name="q_codes%d" % g, align_bytes=64) for g in range(PASSES)]
-        q_scales = [keep.tile([P, NQ], U8, name="q_scales%d" % g, align_bytes=64) for g in range(PASSES)]
-        width = PASSES * 2 * UNIT
-        pages = UNIT // SEG
+        q_codes = keep.tile([P, PASSES * NQ], U32, name="q_codes", align_bytes=64)
+        q_scales = keep.tile([P, PASSES * NQ], U8, name="q_scales", align_bytes=64)
+        starts = [sum(WIDTHS[:u]) for u in range(len(WIDTHS))]
+        totals = keep.tile([P, N], F32, name="totals")
+        first = keep.tile([P, 4 * WIDTHS[0]], U8, name="parted_first", align_bytes=64)
+        rest = keep.tile([P, 4 * (N - WIDTHS[0])], U8, name="parted_rest", tag="raw1", align_bytes=64)
+        parted = [first[:]] + [
+            rest[:, 4 * (s - WIDTHS[0]) : 4 * (s + w - WIDTHS[0])] for s, w in zip(starts[1:], WIDTHS[1:])
+        ]
         scores = {}
-        totals = {}
 
         def gather_words(h):
             nc.vector.tensor_copy(
@@ -115,64 +113,56 @@ def tile_attend_page_prior_kernel(tc, qT, k_words, k_scales, kb, pw, offs, out):
                 word_pool[:].bitcast(U32).indirect(offsets[:, h * cols : (h + 1) * cols]),
             )
 
-        first = keep.tile([P, width], U8, name="parted_first", align_bytes=64)
-        rest = keep.tile([P, (UNITS - 1) * width], U8, name="parted_rest", tag="raw1", align_bytes=64)
-        parted = [first[:]] + [rest[:, u * width : (u + 1) * width] for u in range(UNITS - 1)]
-
         def part(u):
             nc.vector.tensor_copy(
                 parted[u].bitcast(U16).rearrange("p (g n) -> p g n", g=PASSES),
-                got[:, u * UNIT : (u + 1) * UNIT].bitcast(U16).rearrange("p (n g) -> p g n", g=PASSES),
+                got[:, starts[u] : starts[u] + WIDTHS[u]].bitcast(U16).rearrange("p (n g) -> p g n", g=PASSES),
             )
 
         def score(u):
-            keys = parted[u]
-            scores[u] = psum.tile([P, UNIT], F32, name="scores%d" % u)
-            for b in range(UNIT // P):
+            scores[u] = psum.tile([P, 4, P], F32, name="scores%d" % u, tag="bank%d" % u)
+            for b in range(WIDTHS[u] // P):
                 for g in range(PASSES):
-                    c0 = g * 2 * UNIT + 2 * P * b
-                    s0 = g * N + u * UNIT + b * P
+                    c0 = 2 * (g * WIDTHS[u] + P * b)
+                    s0 = g * N + starts[u] + b * P
                     nc.tensor.matmul_mx(
-                        out=scores[u][:, b * P : (b + 1) * P],
-                        lhsT=q_codes[g][:].bitcast(FP8X4),
-                        lhsT_scale=q_scales[g][:],
-                        rhs=keys[:, c0 : c0 + 2 * P].bitcast(FP4X4),
+                        out=scores[u][:, b, :],
+                        lhsT=q_codes[:, g * NQ : (g + 1) * NQ].bitcast(FP8X4),
+                        lhsT_scale=q_scales[:, g * NQ : (g + 1) * NQ],
+                        rhs=parted[u][:, c0 : c0 + 2 * P].bitcast(FP4X4),
                         rhs_scale=planes[:, s0 : s0 + P],
                         start=(g == 0),
                         stop=(g == PASSES - 1),
                     )
 
         def add_bias(u):
-            totals[u] = keep.tile([P, UNIT], F32, name="total%d" % u)
-            c0 = (u % 2) * UNIT
-            nc.vector.tensor_tensor(totals[u][:], scores[u][:], bias_rows[u // 2][:, c0 : c0 + UNIT], add)
+            span = slice(starts[u], starts[u] + WIDTHS[u])
+            sums = scores[u][:, 0 : WIDTHS[u] // P, :].rearrange("p b n -> p (b n)")
+            nc.vector.tensor_tensor(totals[:, span], sums, bias_rows[:, span], add)
 
         def page_max(u):
+            s0, s1 = starts[u], starts[u] + WIDTHS[u]
             nc.vector.tensor_reduce(
-                best[:, u * pages : (u + 1) * pages],
-                totals[u][:].rearrange("p (j s) -> p j s", s=SEG),
+                best[:, s0 // SEG : s1 // SEG],
+                totals[:, s0:s1].rearrange("p (j s) -> p j s", s=SEG),
                 mybir.AxisListType.X,
                 amax,
             )
 
-        def quantize(g):
-            nc.vector.quantize_mx(
-                out=q_codes[g][:].bitcast(FP8X4), scales=q_scales[g][:], in_=q_bf[g][:].rearrange("p w j -> p (w j)")
-            )
-
-        quantize(0)
         gather_words(0)
         gather_words(1)
         part(0)
-        quantize(1)
-        for u in range(UNITS):
+        nc.vector.quantize_mx(
+            out=q_codes[:].bitcast(FP8X4), scales=q_scales[:], in_=q_bf[:].rearrange("p g w j -> p (g w j)")
+        )
+        for u in range(len(WIDTHS)):
             if u > 0:
                 part(u)
             score(u)
         add_bias(0)
-        for u in range(1, UNITS):
+        for u in range(1, len(WIDTHS)):
             add_bias(u)
             page_max(u - 1)
-        page_max(UNITS - 1)
+        page_max(len(WIDTHS) - 1)
         nc.vector.tensor_scalar_mul(result[:], best[:], weight[:])
         nc.sync.dma_start(out=out[0], in_=result[:])

@@ -36,7 +36,7 @@ def tile_attend_page_prior_kernel(tc, qT, k_words, k_scales, kb, pw, offs, out):
         psum = ctx.enter_context(tc.psum_pool(name="psum", bufs=1))
 
         offsets = keep.tile([P, N // 16], U16, name="offsets")
-        word_pool = keep.tile([P, T], I32, name="word_pool", tag="words", align_bytes=64)
+        word_pool = keep.tile([P, T], I32, name="word_pool", align_bytes=64)
         scale_pool = keep.tile([P, T + 4], U8, name="scale_pool", align_bytes=64)
         bias_pool = keep.tile([P, T], F32, name="bias_pool", align_bytes=64)
         scale_got = keep.tile([P, N], U8, name="scale_got", align_bytes=64)
@@ -48,9 +48,8 @@ def tile_attend_page_prior_kernel(tc, qT, k_words, k_scales, kb, pw, offs, out):
         q_raw = [keep.tile([P, 4, NQ], F32, name="q_raw%d" % g, tag="raw%d" % g, align_bytes=64) for g in range(PASSES)]
 
         nc.sync.dma_start(offsets[:], offs)
-        nc.sync.dma_start(
-            out=scale_pool[0:ROWS, 0:T].bitcast(I32), in_=k_scales.bitcast(I32).rearrange("o f t -> f o t")
-        )
+        for g in range(PASSES):
+            nc.sync.dma_start(out=scale_pool[g:ROWS:PASSES, 0:T].bitcast(I32), in_=k_scales[g].bitcast(I32))
         nc.scalar.dma_start(out=bias_pool[P - 1 : P, :], in_=kb[0:1, :])
         q_rows = qT[0].rearrange("(g p j) w -> g p j w", g=PASSES, j=4)
         nc.sync.dma_start(out=word_pool[:], in_=k_words[0].rearrange("p t b -> p (t b)").bitcast(I32))
@@ -88,14 +87,17 @@ def tile_attend_page_prior_kernel(tc, qT, k_words, k_scales, kb, pw, offs, out):
         weight = keep.tile([P, 1], F32, name="weight", tag="column0")
         nc.sync.dma_start(out=weight[:], in_=pw[0])
 
-        q_bf = keep.tile([P, PASSES, NQ, 4], BF16, name="q_bf", tag="half1", align_bytes=64)
+        q_bf = [
+            keep.tile([P, NQ, 4], BF16, name="q_bf%d" % g, tag=["rounded", "half1"][g], align_bytes=64)
+            for g in range(PASSES)
+        ]
         for g in range(PASSES):
-            nc.scalar.copy(q_bf[:, g, :, :], q_raw[g][:].rearrange("p j w -> p w j"))
+            nc.scalar.copy(q_bf[g][:], q_raw[g][:].rearrange("p j w -> p w j"))
         bias_rows = keep.tile([P, N], F32, name="bias_rows")
         for h in range(2):
             nc.scalar.copy(bias_rows[:, h * HALF : (h + 1) * HALF], spread[h][:].rearrange("p b n -> p (b n)"))
 
-        got = keep.tile([P, N], U32, name="word_got", tag="half0", align_bytes=64)
+        got = keep.tile([P, N], U32, name="word_got", align_bytes=64)
         q_codes = keep.tile([P, PASSES * NQ], U32, name="q_codes", align_bytes=64)
         q_scales = keep.tile([P, PASSES * NQ], U8, name="q_scales", align_bytes=64)
         starts = [sum(WIDTHS[:u]) for u in range(len(WIDTHS))]
@@ -152,9 +154,12 @@ def tile_attend_page_prior_kernel(tc, qT, k_words, k_scales, kb, pw, offs, out):
         gather_words(0)
         gather_words(1)
         part(0)
-        nc.vector.quantize_mx(
-            out=q_codes[:].bitcast(FP8X4), scales=q_scales[:], in_=q_bf[:].rearrange("p g w j -> p (g w j)")
-        )
+        for g in range(PASSES):
+            nc.vector.quantize_mx(
+                out=q_codes[:, g * NQ : (g + 1) * NQ].bitcast(FP8X4),
+                scales=q_scales[:, g * NQ : (g + 1) * NQ],
+                in_=q_bf[g][:].rearrange("p w j -> p (w j)"),
+            )
         for u in range(len(WIDTHS)):
             if u > 0:
                 part(u)

@@ -73,7 +73,11 @@ def tile_attend_page_prior_kernel(tc, qT, k_words, k_scales, kb, pw, offs, out):
         spread = []
         for h in range(2):
             bias_got = keep.tile([P, HALF], F32, name="bias_got%d" % h, tag="half%d" % h, align_bytes=64)
-            nc.vector.tensor_copy(bias_got[:], bias_pool[:].indirect(offsets[:, h * cols : (h + 1) * cols]))
+            picked = bias_pool[:].indirect(offsets[:, h * cols : (h + 1) * cols])
+            if h == 0:
+                nc.vector.tensor_copy(bias_got[:], picked)
+            else:
+                nc.scalar.activation(bias_got[:], picked, mybir.ActivationFunctionType.Copy)
             turned = psum.tile([P, 4, P], F32, name="turned%d" % h, tag="bank%d" % h)
             for b in range(4):
                 nc.tensor.transpose(turned[:, b, :], bias_got[:, b * P : (b + 1) * P], ident[:])

@@ -63,7 +63,7 @@ def tile_attend_page_prior_kernel(tc, qT, k_words, k_scales, kb, pw, offs, out):
         nc.vector.memset(scale_pool[64:P, :].bitcast(I32), 0)
 
         nc.vector.tensor_copy(scale_got[:], scale_pool[:, 0:T].indirect(offsets[:]))
-        for quad in range(4):
+        for quad in (0, 2, 1, 3):
             nc.sync.dma_start(
                 out=planes[32 * quad : 32 * quad + 4, :].bitcast(I32),
                 in_=scale_got[8 * quad : 8 * quad + 8, :].bitcast(I32),
@@ -107,9 +107,10 @@ def tile_attend_page_prior_kernel(tc, qT, k_words, k_scales, kb, pw, offs, out):
         starts = [sum(WIDTHS[:u]) for u in range(len(WIDTHS))]
         totals = keep.tile([P, N], F32, name="totals")
         first = keep.tile([P, 4 * WIDTHS[0]], U8, name="parted_first", align_bytes=64)
-        rest = keep.tile([P, 4 * (N - WIDTHS[0])], U8, name="parted_rest", tag="raw1", align_bytes=64)
-        parted = [first[:]] + [
-            rest[:, 4 * (s - WIDTHS[0]) : 4 * (s + w - WIDTHS[0])] for s, w in zip(starts[1:], WIDTHS[1:])
+        second = keep.tile([P, 4 * WIDTHS[1]], U8, name="parted_second", tag="raw0", align_bytes=64)
+        rest = keep.tile([P, 4 * (N - starts[2])], U8, name="parted_rest", tag="raw1", align_bytes=64)
+        parted = [first[:], second[:]] + [
+            rest[:, 4 * (s - starts[2]) : 4 * (s + w - starts[2])] for s, w in zip(starts[2:], WIDTHS[2:])
         ]
         scores = {}
 
@@ -125,26 +126,31 @@ def tile_attend_page_prior_kernel(tc, qT, k_words, k_scales, kb, pw, offs, out):
                 got[:, starts[u] : starts[u] + WIDTHS[u]].bitcast(U16).rearrange("p (n g) -> p g n", g=PASSES),
             )
 
-        def score(u):
-            scores[u] = psum.tile([P, 4, P], F32, name="scores%d" % u, tag="bank%d" % u)
-            for b in range(WIDTHS[u] // P):
-                for g in range(PASSES):
-                    c0 = 2 * (g * WIDTHS[u] + P * b)
-                    s0 = g * N + starts[u] + b * P
-                    nc.tensor.matmul_mx(
-                        out=scores[u][:, b, :],
-                        lhsT=q_codes[:, g * NQ : (g + 1) * NQ].bitcast(FP8X4),
-                        lhsT_scale=q_scales[:, g * NQ : (g + 1) * NQ],
-                        rhs=parted[u][:, c0 : c0 + 2 * P].bitcast(FP4X4),
-                        rhs_scale=planes[:, s0 : s0 + P],
-                        start=(g == 0),
-                        stop=(g == PASSES - 1),
-                    )
+        def score(u, g):
+            if g == 0:
+                scores[u] = psum.tile([P, WIDTHS[u]], F32, name="scores%d" % u, tag="bank%d" % u)
+            c0 = 2 * g * WIDTHS[u]
+            s0 = g * N + starts[u]
+            nc.tensor.matmul_mx(
+                out=scores[u][:],
+                lhsT=q_codes[:, g * NQ : (g + 1) * NQ].bitcast(FP8X4),
+                lhsT_scale=q_scales[:, g * NQ : (g + 1) * NQ],
+                rhs=parted[u][:, c0 : c0 + 2 * WIDTHS[u]].bitcast(FP4X4),
+                rhs_scale=planes[:, s0 : s0 + WIDTHS[u]],
+                start=(g == 0),
+                stop=(g == PASSES - 1),
+            )
+
+        def quantise(g):
+            nc.vector.quantize_mx(
+                out=q_codes[:, g * NQ : (g + 1) * NQ].bitcast(FP8X4),
+                scales=q_scales[:, g * NQ : (g + 1) * NQ],
+                in_=q_bf[g][:].rearrange("p w j -> p (w j)"),
+            )
 
         def add_bias(u):
             span = slice(starts[u], starts[u] + WIDTHS[u])
-            sums = scores[u][:, 0 : WIDTHS[u] // P, :].rearrange("p b n -> p (b n)")
-            nc.vector.tensor_tensor(totals[:, span], sums, bias_rows[:, span], add)
+            nc.vector.tensor_tensor(totals[:, span], scores[u][:], bias_rows[:, span], add)
 
         def page_max(u):
             s0, s1 = starts[u], starts[u] + WIDTHS[u]
@@ -158,16 +164,16 @@ def tile_attend_page_prior_kernel(tc, qT, k_words, k_scales, kb, pw, offs, out):
         gather_words(0)
         gather_words(1)
         part(0)
+        quantise(0)
+        part(1)
+        quantise(1)
         for g in range(PASSES):
-            nc.vector.quantize_mx(
-                out=q_codes[:, g * NQ : (g + 1) * NQ].bitcast(FP8X4),
-                scales=q_scales[:, g * NQ : (g + 1) * NQ],
-                in_=q_bf[g][:].rearrange("p w j -> p (w j)"),
-            )
-        for u in range(len(WIDTHS)):
-            if u > 0:
-                part(u)
-            score(u)
+            for u in range(2):
+                score(u, g)
+        for u in range(2, len(WIDTHS)):
+            part(u)
+            for g in range(PASSES):
+                score(u, g)
         add_bias(0)
         for u in range(1, len(WIDTHS)):
             add_bias(u)

@@ -19,6 +19,7 @@ NQ = 128
 SEG = 32
 HALF = 512
 WIDTHS = [128, 256, 256, 256, 128]
+EARLY = 3
 PASSES = 2
 KP = 512
 ROWS = 32
@@ -96,7 +97,10 @@ def tile_attend_page_prior_kernel(tc, qT, k_words, k_scales, kb, pw, offs, out):
             for g in range(PASSES)
         ]
         for g in range(PASSES):
-            nc.scalar.copy(q_bf[g][:], q_raw[g][:].rearrange("p j w -> p w j"))
+            nc.scalar.copy(
+                q_bf[g][:].rearrange("p (c i) j -> p c j i", i=4),
+                q_raw[g][:].rearrange("p j (c i) -> p c j i", i=4),
+            )
         bias_rows = keep.tile([P, N], F32, name="bias_rows")
         for h in range(2):
             nc.scalar.copy(bias_rows[:, h * HALF : (h + 1) * HALF], spread[h][:].rearrange("p b n -> p (b n)"))
@@ -107,11 +111,12 @@ def tile_attend_page_prior_kernel(tc, qT, k_words, k_scales, kb, pw, offs, out):
         starts = [sum(WIDTHS[:u]) for u in range(len(WIDTHS))]
         totals = keep.tile([P, N], F32, name="totals")
         first = keep.tile([P, 4 * WIDTHS[0]], U8, name="parted_first", align_bytes=64)
-        second = keep.tile([P, 4 * WIDTHS[1]], U8, name="parted_second", tag="raw0", align_bytes=64)
-        rest = keep.tile([P, 4 * (N - starts[2])], U8, name="parted_rest", tag="raw1", align_bytes=64)
-        parted = [first[:], second[:]] + [
-            rest[:, 4 * (s - starts[2]) : 4 * (s + w - starts[2])] for s, w in zip(starts[2:], WIDTHS[2:])
-        ]
+        second = keep.tile([P, 4 * (starts[EARLY] - starts[1])], U8, name="parted_second", tag="raw0", align_bytes=64)
+        rest = keep.tile([P, 4 * (N - starts[EARLY])], U8, name="parted_rest", tag="raw1", align_bytes=64)
+        parted = [first[:]]
+        for u in range(1, len(WIDTHS)):
+            tile, base = (second, starts[1]) if u < EARLY else (rest, starts[EARLY])
+            parted.append(tile[:, 4 * (starts[u] - base) : 4 * (starts[u] + WIDTHS[u] - base)])
         scores = {}
 
         def gather_words(h):
@@ -165,12 +170,13 @@ def tile_attend_page_prior_kernel(tc, qT, k_words, k_scales, kb, pw, offs, out):
         gather_words(1)
         part(0)
         quantise(0)
-        part(1)
+        for u in range(1, EARLY):
+            part(u)
         quantise(1)
         for g in range(PASSES):
-            for u in range(2):
+            for u in range(EARLY):
                 score(u, g)
-        for u in range(2, len(WIDTHS)):
+        for u in range(EARLY, len(WIDTHS)):
             part(u)
             for g in range(PASSES):
                 score(u, g)

@@ -110,13 +110,19 @@ def tile_attend_page_prior_kernel(tc, qT, k_words, k_scales, kb, pw, offs, out):
         q_scales = keep.tile([P, PASSES * NQ], U8, name="q_scales", align_bytes=64)
         starts = [sum(WIDTHS[:u]) for u in range(len(WIDTHS))]
         totals = keep.tile([P, N], F32, name="totals")
-        first = keep.tile([P, 4 * WIDTHS[0]], U8, name="parted_first", align_bytes=64)
-        second = keep.tile([P, 4 * (starts[EARLY] - starts[1])], U8, name="parted_second", tag="raw0", align_bytes=64)
-        rest = keep.tile([P, 4 * (N - starts[EARLY])], U8, name="parted_rest", tag="raw1", align_bytes=64)
-        parted = [first[:]]
-        for u in range(1, len(WIDTHS)):
-            tile, base = (second, starts[1]) if u < EARLY else (rest, starts[EARLY])
-            parted.append(tile[:, 4 * (starts[u] - base) : 4 * (starts[u] + WIDTHS[u] - base)])
+        early = starts[EARLY]
+        before = keep.tile([P, 2 * (early + starts[EARLY - 1])], U8, name="parted_before", tag="raw0", align_bytes=64)
+        after = keep.tile([P, 4 * N - 2 * (early + starts[EARLY - 1])], U8, name="parted_after", tag="raw1", align_bytes=64)
+        moving = {}
+        for u in range(EARLY):
+            moving[u, 0] = before[:, 2 * starts[u] : 2 * (starts[u] + WIDTHS[u])]
+        for u in range(EARLY - 1):
+            moving[u, 1] = before[:, 2 * (early + starts[u]) : 2 * (early + starts[u] + WIDTHS[u])]
+        moving[EARLY - 1, 1] = after[:, 0 : 2 * WIDTHS[EARLY - 1]]
+        for u in range(EARLY, len(WIDTHS)):
+            base = 2 * WIDTHS[EARLY - 1] + 4 * (starts[u] - early)
+            for g in range(PASSES):
+                moving[u, g] = after[:, base + 2 * g * WIDTHS[u] : base + 2 * (g + 1) * WIDTHS[u]]
         scores = {}
 
         def gather_words(h):
@@ -125,22 +131,27 @@ def tile_attend_page_prior_kernel(tc, qT, k_words, k_scales, kb, pw, offs, out):
                 word_pool[:].bitcast(U32).indirect(offsets[:, h * cols : (h + 1) * cols]),
             )
 
+        halves = got[:].bitcast(U16).rearrange("p (n g) -> p g n", g=PASSES)
+
+        def part_pass(dest, g, s0, s1):
+            nc.vector.tensor_copy(dest.bitcast(U16), halves[:, g, s0:s1])
+
         def part(u):
+            base = 2 * WIDTHS[EARLY - 1] + 4 * (starts[u] - early)
             nc.vector.tensor_copy(
-                parted[u].bitcast(U16).rearrange("p (g n) -> p g n", g=PASSES),
-                got[:, starts[u] : starts[u] + WIDTHS[u]].bitcast(U16).rearrange("p (n g) -> p g n", g=PASSES),
+                after[:, base : base + 4 * WIDTHS[u]].bitcast(U16).rearrange("p (g n) -> p g n", g=PASSES),
+                halves[:, :, starts[u] : starts[u] + WIDTHS[u]],
             )
 
         def score(u, g):
             if g == 0:
                 scores[u] = psum.tile([P, WIDTHS[u]], F32, name="scores%d" % u, tag="bank%d" % u)
-            c0 = 2 * g * WIDTHS[u]
             s0 = g * N + starts[u]
             nc.tensor.matmul_mx(
                 out=scores[u][:],
                 lhsT=q_codes[:, g * NQ : (g + 1) * NQ].bitcast(FP8X4),
                 lhsT_scale=q_scales[:, g * NQ : (g + 1) * NQ],
-                rhs=parted[u][:, c0 : c0 + 2 * WIDTHS[u]].bitcast(FP4X4),
+                rhs=moving[u, g].bitcast(FP4X4),
                 rhs_scale=planes[:, s0 : s0 + WIDTHS[u]],
                 start=(g == 0),
                 stop=(g == PASSES - 1),
@@ -168,11 +179,12 @@ def tile_attend_page_prior_kernel(tc, qT, k_words, k_scales, kb, pw, offs, out):
 
         gather_words(0)
         gather_words(1)
-        part(0)
         quantise(0)
-        for u in range(1, EARLY):
-            part(u)
+        for u in range(EARLY):
+            part_pass(moving[u, 0], 0, starts[u], starts[u] + WIDTHS[u])
+        part_pass(before[:, 2 * early :], 1, 0, starts[EARLY - 1])
         quantise(1)
+        part_pass(moving[EARLY - 1, 1], 1, starts[EARLY - 1], early)
         for g in range(PASSES):
             for u in range(EARLY):
                 score(u, g)

@@ -20,9 +20,11 @@ SEG = 32
 HALF = 512
 WIDTHS = [128, 256, 256, 256, 128]
 EARLY = 3
+SHARE = 32
 PASSES = 2
 KP = 512
 ROWS = 32
+SPLIT = 3456
 
 FLOPS = 2 * 1024 * N * NQ
 BYTES = P * T * 4 + 32 * T + 1024 * NQ * 4 + T * 4 + NQ * 4 + P * 64 * 2 + NQ * 32 * 4
@@ -34,6 +36,7 @@ def tile_attend_page_prior_kernel(tc, qT, k_words, k_scales, kb, pw, offs, out):
     amax = mybir.AluOpType.max
     with ExitStack() as ctx:
         keep = ctx.enter_context(tc.tile_pool(name="keep", bufs=1))
+        placed = ctx.enter_context(tc.tile_pool(name="placed", bufs=1))
         psum = ctx.enter_context(tc.psum_pool(name="psum", bufs=1))
 
         offsets = keep.tile([P, N // 16], U16, name="offsets")
@@ -46,7 +49,9 @@ def tile_attend_page_prior_kernel(tc, qT, k_words, k_scales, kb, pw, offs, out):
         ident = keep.tile([P, P], F32, name="ident", align_bytes=64)
         best = keep.tile([P, N // SEG], F32, name="best")
         result = keep.tile([P, N // SEG], F32, name="result")
-        q_raw = [keep.tile([P, 4, NQ], F32, name="q_raw%d" % g, tag="raw%d" % g, align_bytes=64) for g in range(PASSES)]
+        q_raw = [
+            placed.tile([P, 4, NQ], F32, name="q_raw%d" % g, offset=12288 * g, align_bytes=64) for g in range(PASSES)
+        ]
 
         nc.sync.dma_start(offsets[:], offs)
         for g in range(PASSES):
@@ -57,7 +62,10 @@ def tile_attend_page_prior_kernel(tc, qT, k_words, k_scales, kb, pw, offs, out):
         for g in range(PASSES):
             nc.sync.dma_start(out=q_raw[g][:], in_=q_rows[g])
 
-        nc.gpsimd.memset(bias_pool[0 : P - 1, :], 0.0)
+        nc.gpsimd.memset(bias_pool[0 : P - 1, 0:SPLIT], 0.0)
+        middle = (SPLIT + T) // 2 + 1
+        nc.vector.memset(bias_pool[0 : P - 1, SPLIT:middle], 0.0)
+        nc.vector.memset(bias_pool[0 : P - 1, middle:T], 0.0)
         make_identity(nc, ident[:])
         nc.gpsimd.memset(planes[:].bitcast(I32), 0)
         nc.vector.memset(scale_pool[32:64, :].bitcast(I32), 0)
@@ -72,16 +80,13 @@ def tile_attend_page_prior_kernel(tc, qT, k_words, k_scales, kb, pw, offs, out):
 
         cols = HALF // 16
         spread = []
+        bias_got = placed.tile([P, N], F32, name="bias_got", offset=2048, align_bytes=64)
+        nc.scalar.activation(bias_got[:, 0:HALF], bias_pool[:].indirect(offsets[:, 0:cols]), mybir.ActivationFunctionType.Copy)
+        nc.vector.tensor_copy(bias_got[:, HALF:N], bias_pool[:].indirect(offsets[:, cols : 2 * cols]))
         for h in range(2):
-            bias_got = keep.tile([P, HALF], F32, name="bias_got%d" % h, tag="half%d" % h, align_bytes=64)
-            picked = bias_pool[:].indirect(offsets[:, h * cols : (h + 1) * cols])
-            if h == 0:
-                nc.vector.tensor_copy(bias_got[:], picked)
-            else:
-                nc.scalar.activation(bias_got[:], picked, mybir.ActivationFunctionType.Copy)
             turned = psum.tile([P, 4, P], F32, name="turned%d" % h, tag="bank%d" % h)
             for b in range(4):
-                nc.tensor.transpose(turned[:, b, :], bias_got[:, b * P : (b + 1) * P], ident[:])
+                nc.tensor.transpose(turned[:, b, :], bias_got[:, h * HALF + b * P : h * HALF + (b + 1) * P], ident[:])
             nc.scalar.copy(bias_col[h][:], turned[:, :, P - 1])
         for h in range(2):
             bank = psum.tile([P, 4, P], F32, name="spread%d" % h)
@@ -93,15 +98,18 @@ def tile_attend_page_prior_kernel(tc, qT, k_words, k_scales, kb, pw, offs, out):
         nc.sync.dma_start(out=weight[:], in_=pw[0])
 
         q_bf = [
-            keep.tile([P, NQ, 4], BF16, name="q_bf%d" % g, tag=["rounded", "half1"][g], align_bytes=64)
+            placed.tile([P, NQ, 4], BF16, name="q_bf%d" % g, offset=4096 + 1024 * g, align_bytes=64)
             for g in range(PASSES)
         ]
-        for g in range(PASSES):
-            nc.scalar.copy(
-                q_bf[g][:].rearrange("p (c i) j -> p c j i", i=4),
-                q_raw[g][:].rearrange("p j (c i) -> p c j i", i=4),
+        def rounding(g, w0, w1):
+            return (
+                q_bf[g][:, w0:w1, :].rearrange("p (c i) j -> p c j i", i=4),
+                q_raw[g][:, :, w0:w1].rearrange("p j (c i) -> p c j i", i=4),
             )
-        bias_rows = keep.tile([P, N], F32, name="bias_rows")
+
+        nc.scalar.copy(*rounding(0, 0, NQ))
+        nc.scalar.copy(*rounding(1, 0, NQ - SHARE))
+        bias_rows = placed.tile([P, N], F32, name="bias_rows", offset=9216, align_bytes=64)
         for h in range(2):
             nc.scalar.copy(bias_rows[:, h * HALF : (h + 1) * HALF], spread[h][:].rearrange("p b n -> p (b n)"))
 
@@ -111,8 +119,8 @@ def tile_attend_page_prior_kernel(tc, qT, k_words, k_scales, kb, pw, offs, out):
         starts = [sum(WIDTHS[:u]) for u in range(len(WIDTHS))]
         totals = keep.tile([P, N], F32, name="totals")
         early = starts[EARLY]
-        before = keep.tile([P, 2 * (early + starts[EARLY - 1])], U8, name="parted_before", tag="raw0", align_bytes=64)
-        after = keep.tile([P, 4 * N - 2 * (early + starts[EARLY - 1])], U8, name="parted_after", tag="raw1", align_bytes=64)
+        before = placed.tile([P, 2 * (early + starts[EARLY - 1])], U8, name="parted_before", offset=1024, align_bytes=64)
+        after = placed.tile([P, 4 * N - 2 * (early + starts[EARLY - 1])], U8, name="parted_after", offset=13312, align_bytes=64)
         moving = {}
         for u in range(EARLY):
             moving[u, 0] = before[:, 2 * starts[u] : 2 * (starts[u] + WIDTHS[u])]
@@ -179,6 +187,7 @@ def tile_attend_page_prior_kernel(tc, qT, k_words, k_scales, kb, pw, offs, out):
 
         gather_words(0)
         gather_words(1)
+        nc.vector.tensor_copy(*rounding(1, NQ - SHARE, NQ))
         quantise(0)
         for u in range(EARLY):
             part_pass(moving[u, 0], 0, starts[u], starts[u] + WIDTHS[u])

@@ -18,8 +18,8 @@ N = 1024
 NQ = 128
 SEG = 32
 HALF = 512
-WIDTHS = [128, 256, 256, 256, 128]
-EARLY = 3
+WIDTHS = [256, 256, 256, 256]
+EARLY = 2
 SHARE = 32
 PASSES = 2
 KP = 512

@@ -18,13 +18,13 @@ N = 1024
 NQ = 128
 SEG = 32
 HALF = 512
-WIDTHS = [256, 256, 256, 256]
-EARLY = 2
-SHARE = 32
 PASSES = 2
-KP = 512
 ROWS = 32
 SPLIT = 3456
+WIDTHS = [256, 256, 256, 128, 128]
+EARLY = 3
+AHEAD = 2
+HANDED = [1]
 
 FLOPS = 2 * 1024 * N * NQ
 BYTES = P * T * 4 + 32 * T + 1024 * NQ * 4 + T * 4 + NQ * 4 + P * 64 * 2 + NQ * 32 * 4
@@ -34,60 +34,76 @@ def tile_attend_page_prior_kernel(tc, qT, k_words, k_scales, kb, pw, offs, out):
     nc = tc.nc
     add = mybir.AluOpType.add
     amax = mybir.AluOpType.max
+    starts = [sum(WIDTHS[:u]) for u in range(len(WIDTHS) + 1)]
     with ExitStack() as ctx:
         keep = ctx.enter_context(tc.tile_pool(name="keep", bufs=1))
         placed = ctx.enter_context(tc.tile_pool(name="placed", bufs=1))
         psum = ctx.enter_context(tc.psum_pool(name="psum", bufs=1))
 
+        def place(name, shape, dtype, offset):
+            return placed.tile(shape, dtype, name=name, offset=offset, align_bytes=64)
+
         offsets = keep.tile([P, N // 16], U16, name="offsets")
         word_pool = keep.tile([P, T], I32, name="word_pool", align_bytes=64)
-        scale_pool = keep.tile([P, T + 4], U8, name="scale_pool", align_bytes=64)
         bias_pool = keep.tile([P, T], F32, name="bias_pool", align_bytes=64)
         scale_got = keep.tile([P, N], U8, name="scale_got", align_bytes=64)
         planes = keep.tile([P, PASSES * N], U8, name="planes", align_bytes=64)
-        bias_col = [keep.tile([P, HALF // P], F32, name="bias_col%d" % h, tag="column%d" % h) for h in range(2)]
         ident = keep.tile([P, P], F32, name="ident", align_bytes=64)
-        best = keep.tile([P, N // SEG], F32, name="best")
-        result = keep.tile([P, N // SEG], F32, name="result")
-        q_raw = [
-            placed.tile([P, 4, NQ], F32, name="q_raw%d" % g, offset=12288 * g, align_bytes=64) for g in range(PASSES)
-        ]
+        bias_col = [keep.tile([P, HALF // P], F32, name="bias_col%d" % h, tag="column%d" % h) for h in range(2)]
+        scale_pool = place("scale_pool", [P, T + 4], U8, 16384)
+        q_raw = [place("q_raw0", [P, 4, NQ], F32, 0), place("q_raw1", [P, 4, NQ], F32, 16384)]
 
         nc.sync.dma_start(offsets[:], offs)
         for g in range(PASSES):
             nc.sync.dma_start(out=scale_pool[g:ROWS:PASSES, 0:T].bitcast(I32), in_=k_scales[g].bitcast(I32))
         nc.scalar.dma_start(out=bias_pool[P - 1 : P, :], in_=kb[0:1, :])
-        q_rows = qT[0].rearrange("(g p j) w -> g p j w", g=PASSES, j=4)
         nc.sync.dma_start(out=word_pool[:], in_=k_words[0].rearrange("p t b -> p (t b)").bitcast(I32))
-        for g in range(PASSES):
-            nc.sync.dma_start(out=q_raw[g][:], in_=q_rows[g])
+        q_rows = qT[0].rearrange("(g p j) w -> g p j w", g=PASSES, j=4)
+        nc.sync.dma_start(out=q_raw[0][:], in_=q_rows[0])
 
         nc.gpsimd.memset(bias_pool[0 : P - 1, 0:SPLIT], 0.0)
         middle = (SPLIT + T) // 2 + 1
         nc.vector.memset(bias_pool[0 : P - 1, SPLIT:middle], 0.0)
         nc.vector.memset(bias_pool[0 : P - 1, middle:T], 0.0)
-        make_identity(nc, ident[:])
         nc.gpsimd.memset(planes[:].bitcast(I32), 0)
+        make_identity(nc, ident[:])
         nc.vector.memset(scale_pool[32:64, :].bitcast(I32), 0)
         nc.vector.memset(scale_pool[64:P, :].bitcast(I32), 0)
 
         nc.vector.tensor_copy(scale_got[:], scale_pool[:, 0:T].indirect(offsets[:]))
-        for quad in (0, 2, 1, 3):
+
+        def send_both(quad):
             nc.sync.dma_start(
                 out=planes[32 * quad : 32 * quad + 4, :].bitcast(I32),
                 in_=scale_got[8 * quad : 8 * quad + 8, :].bitcast(I32),
             )
 
+        def send_pass(quad, g):
+            nc.sync.dma_start(
+                out=planes[32 * quad : 32 * quad + 4, g * N : (g + 1) * N].bitcast(I32),
+                in_=scale_got[8 * quad + g : 8 * quad + 8 : PASSES, :].bitcast(I32),
+            )
+
+        send_both(0)
+        send_both(2)
+        send_pass(1, 0)
+        send_pass(3, 0)
+        nc.sync.dma_start(out=q_raw[1][:], in_=q_rows[1])
+        send_pass(1, 1)
+        send_pass(3, 1)
+
         cols = HALF // 16
-        spread = []
-        bias_got = placed.tile([P, N], F32, name="bias_got", offset=2048, align_bytes=64)
-        nc.scalar.activation(bias_got[:, 0:HALF], bias_pool[:].indirect(offsets[:, 0:cols]), mybir.ActivationFunctionType.Copy)
+        bias_got = place("bias_got", [P, N], F32, 2048)
+        nc.scalar.activation(
+            bias_got[:, 0:HALF], bias_pool[:].indirect(offsets[:, 0:cols]), mybir.ActivationFunctionType.Copy
+        )
         nc.vector.tensor_copy(bias_got[:, HALF:N], bias_pool[:].indirect(offsets[:, cols : 2 * cols]))
         for h in range(2):
             turned = psum.tile([P, 4, P], F32, name="turned%d" % h, tag="bank%d" % h)
             for b in range(4):
                 nc.tensor.transpose(turned[:, b, :], bias_got[:, h * HALF + b * P : h * HALF + (b + 1) * P], ident[:])
             nc.scalar.copy(bias_col[h][:], turned[:, :, P - 1])
+        spread = []
         for h in range(2):
             bank = psum.tile([P, 4, P], F32, name="spread%d" % h)
             for b in range(4):
@@ -97,73 +113,44 @@ def tile_attend_page_prior_kernel(tc, qT, k_words, k_scales, kb, pw, offs, out):
         weight = keep.tile([P, 1], F32, name="weight", tag="column0")
         nc.sync.dma_start(out=weight[:], in_=pw[0])
 
-        q_bf = [
-            placed.tile([P, NQ, 4], BF16, name="q_bf%d" % g, offset=4096 + 1024 * g, align_bytes=64)
-            for g in range(PASSES)
-        ]
-        def rounding(g, w0, w1):
-            return (
-                q_bf[g][:, w0:w1, :].rearrange("p (c i) j -> p c j i", i=4),
-                q_raw[g][:, :, w0:w1].rearrange("p j (c i) -> p c j i", i=4),
+        q_bf = [place("q_bf%d" % g, [P, NQ, 4], BF16, 4096 + 1024 * g) for g in range(PASSES)]
+        for g in range(PASSES):
+            nc.scalar.copy(
+                q_bf[g][:].rearrange("p (c i) j -> p c j i", i=4),
+                q_raw[g][:].rearrange("p j (c i) -> p c j i", i=4),
             )
-
-        nc.scalar.copy(*rounding(0, 0, NQ))
-        nc.scalar.copy(*rounding(1, 0, NQ - SHARE))
-        bias_rows = placed.tile([P, N], F32, name="bias_rows", offset=9216, align_bytes=64)
+        bias_rows = place("bias_rows", [P, N], F32, 13312)
         for h in range(2):
             nc.scalar.copy(bias_rows[:, h * HALF : (h + 1) * HALF], spread[h][:].rearrange("p b n -> p (b n)"))
 
         got = keep.tile([P, N], U32, name="word_got", align_bytes=64)
         q_codes = keep.tile([P, PASSES * NQ], U32, name="q_codes", align_bytes=64)
         q_scales = keep.tile([P, PASSES * NQ], U8, name="q_scales", align_bytes=64)
-        starts = [sum(WIDTHS[:u]) for u in range(len(WIDTHS))]
-        totals = keep.tile([P, N], F32, name="totals")
         early = starts[EARLY]
-        before = placed.tile([P, 2 * (early + starts[EARLY - 1])], U8, name="parted_before", offset=1024, align_bytes=64)
-        after = placed.tile([P, 4 * N - 2 * (early + starts[EARLY - 1])], U8, name="parted_after", offset=13312, align_bytes=64)
-        moving = {}
-        for u in range(EARLY):
-            moving[u, 0] = before[:, 2 * starts[u] : 2 * (starts[u] + WIDTHS[u])]
-        for u in range(EARLY - 1):
-            moving[u, 1] = before[:, 2 * (early + starts[u]) : 2 * (early + starts[u] + WIDTHS[u])]
-        moving[EARLY - 1, 1] = after[:, 0 : 2 * WIDTHS[EARLY - 1]]
-        for u in range(EARLY, len(WIDTHS)):
-            base = 2 * WIDTHS[EARLY - 1] + 4 * (starts[u] - early)
-            for g in range(PASSES):
-                moving[u, g] = after[:, base + 2 * g * WIDTHS[u] : base + 2 * (g + 1) * WIDTHS[u]]
+        ahead = starts[AHEAD]
+        before = place("parted_before", [P, 2 * (early + ahead)], U8, 1024)
+        after = place("parted_after", [P, 4 * N - 2 * (early + ahead)], U8, 17408)
+
+        def parted(g, s0, s1):
+            if g == 0 and s1 <= early:
+                return before[:, 2 * s0 : 2 * s1]
+            if g == 1 and s1 <= ahead:
+                return before[:, 2 * (early + s0) : 2 * (early + s1)]
+            if g == 0:
+                return after[:, 2 * (s0 - early) : 2 * (s1 - early)]
+            return after[:, 2 * (N - early + s0 - ahead) : 2 * (N - early + s1 - ahead)]
+
+        totals = keep.tile([P, N], F32, name="totals")
+        best = keep.tile([P, N // SEG], F32, name="best")
+        result = keep.tile([P, N // SEG], F32, name="result")
+        halves = got[:].bitcast(U16).rearrange("p (n g) -> p g n", g=PASSES)
         scores = {}
 
-        def gather_words(h):
-            nc.vector.tensor_copy(
-                got[:, h * HALF : (h + 1) * HALF],
-                word_pool[:].bitcast(U32).indirect(offsets[:, h * cols : (h + 1) * cols]),
-            )
+        def gather_words(s0, s1):
+            nc.vector.tensor_copy(got[:, s0:s1], word_pool[:].bitcast(U32).indirect(offsets[:, s0 // 16 : s1 // 16]))
 
-        halves = got[:].bitcast(U16).rearrange("p (n g) -> p g n", g=PASSES)
-
-        def part_pass(dest, g, s0, s1):
-            nc.vector.tensor_copy(dest.bitcast(U16), halves[:, g, s0:s1])
-
-        def part(u):
-            base = 2 * WIDTHS[EARLY - 1] + 4 * (starts[u] - early)
-            nc.vector.tensor_copy(
-                after[:, base : base + 4 * WIDTHS[u]].bitcast(U16).rearrange("p (g n) -> p g n", g=PASSES),
-                halves[:, :, starts[u] : starts[u] + WIDTHS[u]],
-            )
-
-        def score(u, g):
-            if g == 0:
-                scores[u] = psum.tile([P, WIDTHS[u]], F32, name="scores%d" % u, tag="bank%d" % u)
-            s0 = g * N + starts[u]
-            nc.tensor.matmul_mx(
-                out=scores[u][:],
-                lhsT=q_codes[:, g * NQ : (g + 1) * NQ].bitcast(FP8X4),
-                lhsT_scale=q_scales[:, g * NQ : (g + 1) * NQ],
-                rhs=moving[u, g].bitcast(FP4X4),
-                rhs_scale=planes[:, s0 : s0 + WIDTHS[u]],
-                start=(g == 0),
-                stop=(g == PASSES - 1),
-            )
+        def part(g, s0, s1):
+            nc.vector.tensor_copy(parted(g, s0, s1).bitcast(U16), halves[:, g, s0:s1])
 
         def quantise(g):
             nc.vector.quantize_mx(
@@ -172,12 +159,31 @@ def tile_attend_page_prior_kernel(tc, qT, k_words, k_scales, kb, pw, offs, out):
                 in_=q_bf[g][:].rearrange("p w j -> p (w j)"),
             )
 
-        def add_bias(u):
-            span = slice(starts[u], starts[u] + WIDTHS[u])
-            nc.vector.tensor_tensor(totals[:, span], scores[u][:], bias_rows[:, span], add)
+        def score(u, g):
+            s0, s1 = starts[u], starts[u + 1]
+            if g == 0:
+                scores[u] = psum.tile([P, s1 - s0], F32, name="scores%d" % u, tag="bank%d" % u)
+            nc.tensor.matmul_mx(
+                out=scores[u][:],
+                lhsT=q_codes[:, g * NQ : (g + 1) * NQ].bitcast(FP8X4),
+                lhsT_scale=q_scales[:, g * NQ : (g + 1) * NQ],
+                rhs=parted(g, s0, s1).bitcast(FP4X4),
+                rhs_scale=planes[:, g * N + s0 : g * N + s1],
+                start=(g == 0),
+                stop=(g == PASSES - 1),
+            )
 
-        def page_max(u):
-            s0, s1 = starts[u], starts[u] + WIDTHS[u]
+        def add_bias(u):
+            s0, s1 = starts[u], starts[u + 1]
+            rows = bias_rows[:, s0:s1]
+            if u in HANDED:
+                plain = keep.tile([P, s1 - s0], F32, name="plain%d" % u)
+                nc.scalar.copy(plain[:], scores[u][:])
+                nc.gpsimd.tensor_tensor(totals[:, s0:s1], plain[:], rows, add)
+            else:
+                nc.vector.tensor_tensor(totals[:, s0:s1], scores[u][:], rows, add)
+
+        def page_max(s0, s1):
             nc.vector.tensor_reduce(
                 best[:, s0 // SEG : s1 // SEG],
                 totals[:, s0:s1].rearrange("p (j s) -> p j s", s=SEG),
@@ -185,26 +191,29 @@ def tile_attend_page_prior_kernel(tc, qT, k_words, k_scales, kb, pw, offs, out):
                 amax,
             )
 
-        gather_words(0)
-        gather_words(1)
-        nc.vector.tensor_copy(*rounding(1, NQ - SHARE, NQ))
+        gather_words(0, HALF)
+        gather_words(HALF, N)
         quantise(0)
         for u in range(EARLY):
-            part_pass(moving[u, 0], 0, starts[u], starts[u] + WIDTHS[u])
-        part_pass(before[:, 2 * early :], 1, 0, starts[EARLY - 1])
+            part(0, starts[u], starts[u + 1])
+            score(u, 0)
+        part(1, 0, ahead)
         quantise(1)
-        part_pass(moving[EARLY - 1, 1], 1, starts[EARLY - 1], early)
+        for u in range(AHEAD):
+            score(u, 1)
+        for u in range(AHEAD, EARLY):
+            part(1, starts[u], starts[u + 1])
+            score(u, 1)
         for g in range(PASSES):
-            for u in range(EARLY):
-                score(u, g)
+            part(g, early, N)
         for u in range(EARLY, len(WIDTHS)):
-            part(u)
             for g in range(PASSES):
                 score(u, g)
-        add_bias(0)
-        for u in range(1, len(WIDTHS)):
+        for u in range(len(WIDTHS)):
             add_bias(u)
-            page_max(u - 1)
-        page_max(len(WIDTHS) - 1)
+        page_max(0, starts[1])
+        page_max(starts[2], starts[3])
+        page_max(starts[1], starts[2])
+        page_max(starts[3], N)
         nc.vector.tensor_scalar_mul(result[:], best[:], weight[:])
         nc.sync.dma_start(out=out[0], in_=result[:])

@@ -78,19 +78,9 @@ def tile_attend_page_prior_kernel(tc, qT, k_words, k_scales, kb, pw, offs, out):
                 in_=scale_got[8 * quad : 8 * quad + 8, :].bitcast(I32),
             )
 
-        def send_pass(quad, g):
-            nc.sync.dma_start(
-                out=planes[32 * quad : 32 * quad + 4, g * N : (g + 1) * N].bitcast(I32),
-                in_=scale_got[8 * quad + g : 8 * quad + 8 : PASSES, :].bitcast(I32),
-            )
-
-        send_both(0)
-        send_both(2)
-        send_pass(1, 0)
-        send_pass(3, 0)
         nc.sync.dma_start(out=q_raw[1][:], in_=q_rows[1])
-        send_pass(1, 1)
-        send_pass(3, 1)
+        for quad in (0, 2, 1, 3):
+            send_both(quad)
 
         cols = HALF // 16
         bias_got = place("bias_got", [P, N], F32, 2048)

@@ -22,9 +22,10 @@ PASSES = 2
 ROWS = 32
 SPLIT = 3456
 WIDTHS = [256, 256, 256, 128, 128]
-EARLY = 3
-AHEAD = 2
-HANDED = [1]
+EARLY = 2
+AHEAD = 1
+GROUP = 256
+HELP = 48
 
 FLOPS = 2 * 1024 * N * NQ
 BYTES = P * T * 4 + 32 * T + 1024 * NQ * 4 + T * 4 + NQ * 4 + P * 64 * 2 + NQ * 32 * 4
@@ -50,7 +51,7 @@ def tile_attend_page_prior_kernel(tc, qT, k_words, k_scales, kb, pw, offs, out):
         planes = keep.tile([P, PASSES * N], U8, name="planes", align_bytes=64)
         ident = keep.tile([P, P], F32, name="ident", align_bytes=64)
         bias_col = [keep.tile([P, HALF // P], F32, name="bias_col%d" % h, tag="column%d" % h) for h in range(2)]
-        scale_pool = place("scale_pool", [P, T + 4], U8, 16384)
+        scale_pool = keep.tile([P, T + 4], U8, name="scale_pool", align_bytes=64)
         q_raw = [place("q_raw0", [P, 4, NQ], F32, 0), place("q_raw1", [P, 4, NQ], F32, 16384)]
 
         nc.sync.dma_start(offsets[:], offs)
@@ -59,14 +60,15 @@ def tile_attend_page_prior_kernel(tc, qT, k_words, k_scales, kb, pw, offs, out):
         nc.scalar.dma_start(out=bias_pool[P - 1 : P, :], in_=kb[0:1, :])
         nc.sync.dma_start(out=word_pool[:], in_=k_words[0].rearrange("p t b -> p (t b)").bitcast(I32))
         q_rows = qT[0].rearrange("(g p j) w -> g p j w", g=PASSES, j=4)
-        nc.sync.dma_start(out=q_raw[0][:], in_=q_rows[0])
+        for g in range(PASSES):
+            nc.sync.dma_start(out=q_raw[g][:], in_=q_rows[g])
 
         nc.gpsimd.memset(bias_pool[0 : P - 1, 0:SPLIT], 0.0)
         middle = (SPLIT + T) // 2 + 1
         nc.vector.memset(bias_pool[0 : P - 1, SPLIT:middle], 0.0)
         nc.vector.memset(bias_pool[0 : P - 1, middle:T], 0.0)
-        nc.gpsimd.memset(planes[:].bitcast(I32), 0)
         make_identity(nc, ident[:])
+        nc.gpsimd.memset(planes[:].bitcast(I32), 0)
         nc.vector.memset(scale_pool[32:64, :].bitcast(I32), 0)
         nc.vector.memset(scale_pool[64:P, :].bitcast(I32), 0)
 
@@ -78,7 +80,6 @@ def tile_attend_page_prior_kernel(tc, qT, k_words, k_scales, kb, pw, offs, out):
                 in_=scale_got[8 * quad : 8 * quad + 8, :].bitcast(I32),
             )
 
-        nc.sync.dma_start(out=q_raw[1][:], in_=q_rows[1])
         for quad in (0, 2, 1, 3):
             send_both(quad)
 
@@ -104,11 +105,16 @@ def tile_attend_page_prior_kernel(tc, qT, k_words, k_scales, kb, pw, offs, out):
         nc.sync.dma_start(out=weight[:], in_=pw[0])
 
         q_bf = [place("q_bf%d" % g, [P, NQ, 4], BF16, 4096 + 1024 * g) for g in range(PASSES)]
-        for g in range(PASSES):
-            nc.scalar.copy(
-                q_bf[g][:].rearrange("p (c i) j -> p c j i", i=4),
-                q_raw[g][:].rearrange("p j (c i) -> p c j i", i=4),
+
+        def rounding(g, w0, w1):
+            return (
+                q_bf[g][:, w0:w1, :].rearrange("p (c i) j -> p c j i", i=4),
+                q_raw[g][:, :, w0:w1].rearrange("p j (c i) -> p c j i", i=4),
             )
+
+        nc.scalar.copy(*rounding(0, 0, NQ - HELP))
+        nc.gpsimd.tensor_scalar(*rounding(0, NQ - HELP, NQ), 1.0, 0.0, mybir.AluOpType.mult, add)
+        nc.scalar.copy(*rounding(1, 0, NQ))
         bias_rows = place("bias_rows", [P, N], F32, 13312)
         for h in range(2):
             nc.scalar.copy(bias_rows[:, h * HALF : (h + 1) * HALF], spread[h][:].rearrange("p b n -> p (b n)"))
@@ -126,9 +132,11 @@ def tile_attend_page_prior_kernel(tc, qT, k_words, k_scales, kb, pw, offs, out):
                 return before[:, 2 * s0 : 2 * s1]
             if g == 1 and s1 <= ahead:
                 return before[:, 2 * (early + s0) : 2 * (early + s1)]
-            if g == 0:
-                return after[:, 2 * (s0 - early) : 2 * (s1 - early)]
-            return after[:, 2 * (N - early + s0 - ahead) : 2 * (N - early + s1 - ahead)]
+            if s1 <= early:
+                return after[:, 2 * (s0 - ahead) : 2 * (s1 - ahead)]
+            first = s0 - (s0 - early) % GROUP
+            base = early - ahead + 2 * (first - early) + g * GROUP - first
+            return after[:, 2 * (base + s0) : 2 * (base + s1)]
 
         totals = keep.tile([P, N], F32, name="totals")
         best = keep.tile([P, N // SEG], F32, name="best")
@@ -141,6 +149,13 @@ def tile_attend_page_prior_kernel(tc, qT, k_words, k_scales, kb, pw, offs, out):
 
         def part(g, s0, s1):
             nc.vector.tensor_copy(parted(g, s0, s1).bitcast(U16), halves[:, g, s0:s1])
+
+        def part_group(s0):
+            base = early - ahead + 2 * (s0 - early)
+            nc.vector.tensor_copy(
+                after[:, 2 * base : 2 * (base + 2 * GROUP)].bitcast(U16).rearrange("p (g n) -> p g n", g=PASSES),
+                halves[:, :, s0 : s0 + GROUP],
+            )
 
         def quantise(g):
             nc.vector.quantize_mx(
@@ -166,12 +181,7 @@ def tile_attend_page_prior_kernel(tc, qT, k_words, k_scales, kb, pw, offs, out):
         def add_bias(u):
             s0, s1 = starts[u], starts[u + 1]
             rows = bias_rows[:, s0:s1]
-            if u in HANDED:
-                plain = keep.tile([P, s1 - s0], F32, name="plain%d" % u)
-                nc.scalar.copy(plain[:], scores[u][:])
-                nc.gpsimd.tensor_tensor(totals[:, s0:s1], plain[:], rows, add)
-            else:
-                nc.vector.tensor_tensor(totals[:, s0:s1], scores[u][:], rows, add)
+            nc.vector.tensor_tensor(totals[:, s0:s1], scores[u][:], rows, add)
 
         def page_max(s0, s1):
             nc.vector.tensor_reduce(
@@ -194,16 +204,19 @@ def tile_attend_page_prior_kernel(tc, qT, k_words, k_scales, kb, pw, offs, out):
         for u in range(AHEAD, EARLY):
             part(1, starts[u], starts[u + 1])
             score(u, 1)
-        for g in range(PASSES):
-            part(g, early, N)
+        for s0 in range(early, N, GROUP):
+            part_group(s0)
         for u in range(EARLY, len(WIDTHS)):
             for g in range(PASSES):
                 score(u, g)
-        for u in range(len(WIDTHS)):
-            add_bias(u)
+        add_bias(0)
+        add_bias(1)
         page_max(0, starts[1])
-        page_max(starts[2], starts[3])
+        add_bias(2)
         page_max(starts[1], starts[2])
+        add_bias(3)
+        add_bias(4)
+        page_max(starts[2], starts[3])
         page_max(starts[3], N)
         nc.vector.tensor_scalar_mul(result[:], best[:], weight[:])
         nc.sync.dma_start(out=out[0], in_=result[:])

@@ -80,8 +80,19 @@ def tile_attend_page_prior_kernel(tc, qT, k_words, k_scales, kb, pw, offs, out):
                 in_=scale_got[8 * quad : 8 * quad + 8, :].bitcast(I32),
             )
 
-        for quad in (0, 2, 1, 3):
-            send_both(quad)
+        def send_half(quad, h):
+            nc.sync.dma_start(
+                out=planes[32 * quad : 32 * quad + 4, :]
+                .bitcast(I32)
+                .rearrange("p (g n) -> p g n", g=PASSES)[:, :, h * HALF // 4 : (h + 1) * HALF // 4],
+                in_=scale_got[8 * quad : 8 * quad + 8, h * HALF : (h + 1) * HALF].bitcast(I32),
+            )
+
+        send_both(0)
+        send_both(2)
+        for h in range(2):
+            send_half(1, h)
+            send_half(3, h)
 
         cols = HALF // 16
         bias_got = place("bias_got", [P, N], F32, 2048)

@@ -63,6 +63,10 @@ def tile_attend_page_prior_kernel(tc, qT, k_words, k_scales, kb, pw, offs, out):
         for g in range(PASSES):
             nc.sync.dma_start(out=q_raw[g][:], in_=q_rows[g])
 
+        spare = keep.tile([P, 16], F32, name="spare")
+        nc.vector.memset(spare[:, 0:1], 0.0)
+        nc.scalar.copy(spare[:, 8:9], spare[:, 0:1])
+
         nc.gpsimd.memset(bias_pool[0 : P - 1, 0:SPLIT], 0.0)
         middle = (SPLIT + T) // 2 + 1
         nc.vector.memset(bias_pool[0 : P - 1, SPLIT:middle], 0.0)

@@ -21,10 +21,10 @@ HALF = 512
 PASSES = 2
 ROWS = 32
 SPLIT = 3456
-WIDTHS = [256, 256, 256, 128, 128]
-EARLY = 2
-AHEAD = 1
-GROUP = 256
+TILES = 4
+RUN = SEG // TILES
+LEAD = 256
+UNITS = [(0, LEAD), (LEAD + HALF, LEAD + HALF + P), (LEAD + HALF + P, N)]
 HELP = 48
 
 FLOPS = 2 * 1024 * N * NQ
@@ -35,7 +35,6 @@ def tile_attend_page_prior_kernel(tc, qT, k_words, k_scales, kb, pw, offs, out):
     nc = tc.nc
     add = mybir.AluOpType.add
     amax = mybir.AluOpType.max
-    starts = [sum(WIDTHS[:u]) for u in range(len(WIDTHS) + 1)]
     with ExitStack() as ctx:
         keep = ctx.enter_context(tc.tile_pool(name="keep", bufs=1))
         placed = ctx.enter_context(tc.tile_pool(name="placed", bufs=1))
@@ -44,13 +43,17 @@ def tile_attend_page_prior_kernel(tc, qT, k_words, k_scales, kb, pw, offs, out):
         def place(name, shape, dtype, offset):
             return placed.tile(shape, dtype, name=name, offset=offset, align_bytes=64)
 
+        def bank(name, shape, number):
+            return psum.tile(shape, F32, name=name, tag="bank%d" % number)
+
         offsets = keep.tile([P, N // 16], U16, name="offsets")
         word_pool = keep.tile([P, T], I32, name="word_pool", align_bytes=64)
         bias_pool = keep.tile([P, T], F32, name="bias_pool", align_bytes=64)
-        scale_got = keep.tile([P, N], U8, name="scale_got", align_bytes=64)
+        scale_got = place("scale_got", [P, N], U8, 20480)
+        scale_dealt = keep.tile([P, N], U8, name="scale_dealt", align_bytes=64)
         planes = keep.tile([P, PASSES * N], U8, name="planes", align_bytes=64)
         ident = keep.tile([P, P], F32, name="ident", align_bytes=64)
-        bias_col = [keep.tile([P, HALF // P], F32, name="bias_col%d" % h, tag="column%d" % h) for h in range(2)]
+        bias_col = [place("bias_col0", [P, 4], F32, 16448), keep.tile([P, 4], F32, name="bias_col1", tag="column1")]
         scale_pool = keep.tile([P, T + 4], U8, name="scale_pool", align_bytes=64)
         q_raw = [place("q_raw0", [P, 4, NQ], F32, 0), place("q_raw1", [P, 4, NQ], F32, 16384)]
 
@@ -77,11 +80,19 @@ def tile_attend_page_prior_kernel(tc, qT, k_words, k_scales, kb, pw, offs, out):
         nc.vector.memset(scale_pool[64:P, :].bitcast(I32), 0)
 
         nc.vector.tensor_copy(scale_got[:], scale_pool[:, 0:T].indirect(offsets[:]))
+        nc.vector.tensor_copy(
+            scale_dealt[0:ROWS, LEAD : LEAD + HALF].bitcast(I32).rearrange("p (r j c) -> p j r c", r=TILES, c=RUN // 4),
+            scale_got[0:ROWS, LEAD : LEAD + HALF].bitcast(I32).rearrange("p (j r c) -> p j r c", r=TILES, c=RUN // 4),
+        )
+        nc.vector.tensor_copy(
+            scale_dealt[0:ROWS, :].bitcast(I32).rearrange("p (a n) -> p a n", a=4)[:, 0:4:3, :],
+            scale_got[0:ROWS, :].bitcast(I32).rearrange("p (a n) -> p a n", a=4)[:, 0:4:3, :],
+        )
 
         def send_both(quad):
             nc.sync.dma_start(
                 out=planes[32 * quad : 32 * quad + 4, :].bitcast(I32),
-                in_=scale_got[8 * quad : 8 * quad + 8, :].bitcast(I32),
+                in_=scale_dealt[8 * quad : 8 * quad + 8, :].bitcast(I32),
             )
 
         def send_half(quad, h):
@@ -89,7 +100,7 @@ def tile_attend_page_prior_kernel(tc, qT, k_words, k_scales, kb, pw, offs, out):
                 out=planes[32 * quad : 32 * quad + 4, :]
                 .bitcast(I32)
                 .rearrange("p (g n) -> p g n", g=PASSES)[:, :, h * HALF // 4 : (h + 1) * HALF // 4],
-                in_=scale_got[8 * quad : 8 * quad + 8, h * HALF : (h + 1) * HALF].bitcast(I32),
+                in_=scale_dealt[8 * quad : 8 * quad + 8, h * HALF : (h + 1) * HALF].bitcast(I32),
             )
 
         send_both(0)
@@ -98,28 +109,42 @@ def tile_attend_page_prior_kernel(tc, qT, k_words, k_scales, kb, pw, offs, out):
             send_half(1, h)
             send_half(3, h)
 
-        cols = HALF // 16
-        bias_got = place("bias_got", [P, N], F32, 2048)
+        bias_first = place("bias_first", [P, HALF], F32, 8192)
+        bias_second = place("bias_second", [P, HALF], F32, 2560)
+        bias_dealt = place("bias_dealt", [P, HALF], F32, 6144)
+        for h, s0 in enumerate((0, LEAD + HALF)):
+            nc.scalar.activation(
+                bias_second[:, h * LEAD : (h + 1) * LEAD],
+                bias_pool[:].indirect(offsets[:, s0 // 16 : (s0 + LEAD) // 16]),
+                mybir.ActivationFunctionType.Copy,
+            )
         nc.scalar.activation(
-            bias_got[:, 0:HALF], bias_pool[:].indirect(offsets[:, 0:cols]), mybir.ActivationFunctionType.Copy
+            bias_first[:],
+            bias_pool[:].indirect(offsets[:, LEAD // 16 : (LEAD + HALF) // 16]),
+            mybir.ActivationFunctionType.Copy,
         )
-        nc.vector.tensor_copy(bias_got[:, HALF:N], bias_pool[:].indirect(offsets[:, cols : 2 * cols]))
-        for h in range(2):
-            turned = psum.tile([P, 4, P], F32, name="turned%d" % h, tag="bank%d" % h)
-            for b in range(4):
-                nc.tensor.transpose(turned[:, b, :], bias_got[:, h * HALF + b * P : h * HALF + (b + 1) * P], ident[:])
-            nc.scalar.copy(bias_col[h][:], turned[:, :, P - 1])
-        spread = []
-        for h in range(2):
-            bank = psum.tile([P, 4, P], F32, name="spread%d" % h)
-            for b in range(4):
-                nc.tensor.transpose(bank[:, b, :], bias_col[h][:, b : b + 1].to_broadcast([P, P]), ident[:])
-            spread.append(bank)
+        nc.gpsimd.tensor_scalar(
+            bias_dealt[:].rearrange("p (r j c) -> p r j c", r=TILES, c=RUN),
+            bias_first[:].rearrange("p (j r c) -> p r j c", r=TILES, c=RUN),
+            1.0,
+            0.0,
+            mybir.AluOpType.mult,
+            add,
+        )
+        turned = [bank("turned%d" % h, [P, 4, P], h) for h in range(2)]
+        for b in range(4):
+            nc.tensor.transpose(turned[1][:, b, :], bias_second[:, b * P : (b + 1) * P], ident[:])
+        nc.scalar.copy(bias_col[1][:], turned[1][:, :, P - 1])
+        spread = bank("spread", [P, 4, P], 7)
+        for b in range(4):
+            nc.tensor.transpose(spread[:, b, :], bias_col[1][:, b : b + 1].to_broadcast([P, P]), ident[:])
+        for b in range(4):
+            nc.tensor.transpose(turned[0][:, b, :], bias_dealt[:, b * P : (b + 1) * P], ident[:])
 
-        weight = keep.tile([P, 1], F32, name="weight", tag="column0")
+        weight = keep.tile([P, 1], F32, name="weight", tag="column1")
         nc.sync.dma_start(out=weight[:], in_=pw[0])
 
-        q_bf = [place("q_bf%d" % g, [P, NQ, 4], BF16, 4096 + 1024 * g) for g in range(PASSES)]
+        q_bf = [place("q_bf0", [P, NQ, 4], BF16, 3072), place("q_bf1", [P, NQ, 4], BF16, 4096)]
 
         def rounding(g, w0, w1):
             return (
@@ -130,46 +155,55 @@ def tile_attend_page_prior_kernel(tc, qT, k_words, k_scales, kb, pw, offs, out):
         nc.scalar.copy(*rounding(0, 0, NQ - HELP))
         nc.gpsimd.tensor_scalar(*rounding(0, NQ - HELP, NQ), 1.0, 0.0, mybir.AluOpType.mult, add)
         nc.scalar.copy(*rounding(1, 0, NQ))
-        bias_rows = place("bias_rows", [P, N], F32, 13312)
-        for h in range(2):
-            nc.scalar.copy(bias_rows[:, h * HALF : (h + 1) * HALF], spread[h][:].rearrange("p b n -> p (b n)"))
+        nc.scalar.copy(bias_col[0][:], turned[0][:, :, P - 1])
+        bias_rows = place("bias_rows", [P, HALF], F32, 16512)
+        nc.scalar.copy(bias_rows[:], spread[:].rearrange("p b n -> p (b n)"))
 
-        got = keep.tile([P, N], U32, name="word_got", align_bytes=64)
+        got = place("word_got", [P, N], U32, 20480)
         q_codes = keep.tile([P, PASSES * NQ], U32, name="q_codes", align_bytes=64)
         q_scales = keep.tile([P, PASSES * NQ], U8, name="q_scales", align_bytes=64)
-        early = starts[EARLY]
-        ahead = starts[AHEAD]
-        before = place("parted_before", [P, 2 * (early + ahead)], U8, 1024)
-        after = place("parted_after", [P, 4 * N - 2 * (early + ahead)], U8, 17408)
+        before = place("parted_before", [P, 4 * HALF], U8, 1024)
+        after = place("parted_after", [P, 4 * HALF], U8, 14400)
 
         def parted(g, s0, s1):
-            if g == 0 and s1 <= early:
-                return before[:, 2 * s0 : 2 * s1]
-            if g == 1 and s1 <= ahead:
-                return before[:, 2 * (early + s0) : 2 * (early + s1)]
-            if s1 <= early:
-                return after[:, 2 * (s0 - ahead) : 2 * (s1 - ahead)]
-            first = s0 - (s0 - early) % GROUP
-            base = early - ahead + 2 * (first - early) + g * GROUP - first
-            return after[:, 2 * (base + s0) : 2 * (base + s1)]
+            tile = before if s0 < HALF else after
+            first = s0 - s0 % LEAD
+            base = 2 * (first % HALF) + g * LEAD - first
+            return tile[:, 2 * (base + s0) : 2 * (base + s1)]
 
-        totals = keep.tile([P, N], F32, name="totals")
+        totals = keep.tile([P, HALF], F32, name="totals")
+        started = keep.tile([P, 2, NQ], F32, name="started")
+        folded = keep.tile([P, 2, NQ], F32, name="folded", align_bytes=64)
         best = keep.tile([P, N // SEG], F32, name="best")
         result = keep.tile([P, N // SEG], F32, name="result")
         halves = got[:].bitcast(U16).rearrange("p (n g) -> p g n", g=PASSES)
+        tiles = {}
         scores = {}
 
         def gather_words(s0, s1):
             nc.vector.tensor_copy(got[:, s0:s1], word_pool[:].bitcast(U32).indirect(offsets[:, s0 // 16 : s1 // 16]))
 
-        def part(g, s0, s1):
-            nc.vector.tensor_copy(parted(g, s0, s1).bitcast(U16), halves[:, g, s0:s1])
+        by_tile = halves[:, :, LEAD : LEAD + HALF].rearrange("p g (j r c) -> p g r j c", r=TILES, c=RUN)
 
-        def part_group(s0):
-            base = early - ahead + 2 * (s0 - early)
+        def part(g):
+            nc.vector.tensor_copy(parted(g, 0, LEAD).bitcast(U16), halves[:, g, 0:LEAD])
+
+        def deal(g):
             nc.vector.tensor_copy(
-                after[:, 2 * base : 2 * (base + 2 * GROUP)].bitcast(U16).rearrange("p (g n) -> p g n", g=PASSES),
-                halves[:, :, s0 : s0 + GROUP],
+                parted(g, LEAD, HALF).bitcast(U16).rearrange("p (r j c) -> p r j c", r=2, c=RUN),
+                by_tile[:, g, 0:2, :, :],
+            )
+
+        def deal_both():
+            nc.vector.tensor_copy(
+                after[:, 0 : 4 * LEAD].bitcast(U16).rearrange("p (g r j c) -> p g r j c", g=PASSES, r=2, c=RUN),
+                by_tile[:, :, 2:4, :, :],
+            )
+
+        def part_both():
+            nc.vector.tensor_copy(
+                after[:, 4 * LEAD : 8 * LEAD].bitcast(U16).rearrange("p (g n) -> p g n", g=PASSES),
+                halves[:, :, LEAD + HALF : N],
             )
 
         def quantise(g):
@@ -179,10 +213,24 @@ def tile_attend_page_prior_kernel(tc, qT, k_words, k_scales, kb, pw, offs, out):
                 in_=q_bf[g][:].rearrange("p w j -> p (w j)"),
             )
 
-        def score(u, g):
-            s0, s1 = starts[u], starts[u + 1]
+        def score_tile(r, g):
+            s0 = LEAD + r * P
             if g == 0:
-                scores[u] = psum.tile([P, s1 - s0], F32, name="scores%d" % u, tag="bank%d" % u)
+                tiles[r] = bank("tile%d" % r, [P, NQ], TILES - 1 - r)
+            nc.tensor.matmul_mx(
+                out=tiles[r][:],
+                lhsT=parted(g, s0, s0 + P).bitcast(FP4X4),
+                lhsT_scale=planes[:, g * N + s0 : g * N + s0 + P],
+                rhs=q_codes[:, g * NQ : (g + 1) * NQ].bitcast(FP8X4),
+                rhs_scale=q_scales[:, g * NQ : (g + 1) * NQ],
+                start=(g == 0),
+                stop=(g == PASSES - 1),
+            )
+
+        def score(u, g):
+            s0, s1 = UNITS[u]
+            if g == 0:
+                scores[u] = bank("scores%d" % u, [P, s1 - s0], TILES + u)
             nc.tensor.matmul_mx(
                 out=scores[u][:],
                 lhsT=q_codes[:, g * NQ : (g + 1) * NQ].bitcast(FP8X4),
@@ -194,14 +242,15 @@ def tile_attend_page_prior_kernel(tc, qT, k_words, k_scales, kb, pw, offs, out):
             )
 
         def add_bias(u):
-            s0, s1 = starts[u], starts[u + 1]
-            rows = bias_rows[:, s0:s1]
-            nc.vector.tensor_tensor(totals[:, s0:s1], scores[u][:], rows, add)
+            s0, s1 = (s - HALF * min(u, 1) for s in UNITS[u])
+            nc.vector.tensor_tensor(totals[:, s0:s1], scores[u][:], bias_rows[:, s0:s1], add)
 
-        def page_max(s0, s1):
+        def page_max(u):
+            s0, s1 = UNITS[u]
+            shift = HALF * min(u, 1)
             nc.vector.tensor_reduce(
                 best[:, s0 // SEG : s1 // SEG],
-                totals[:, s0:s1].rearrange("p (j s) -> p j s", s=SEG),
+                totals[:, s0 - shift : s1 - shift].rearrange("p (j s) -> p j s", s=SEG),
                 mybir.AxisListType.X,
                 amax,
             )
@@ -209,29 +258,47 @@ def tile_attend_page_prior_kernel(tc, qT, k_words, k_scales, kb, pw, offs, out):
         gather_words(0, HALF)
         gather_words(HALF, N)
         quantise(0)
-        for u in range(EARLY):
-            part(0, starts[u], starts[u + 1])
-            score(u, 0)
-        part(1, 0, ahead)
+        part(0)
+        score(0, 0)
+        deal(0)
+        score_tile(0, 0)
+        score_tile(1, 0)
+        part(1)
+        deal(1)
         quantise(1)
-        for u in range(AHEAD):
-            score(u, 1)
-        for u in range(AHEAD, EARLY):
-            part(1, starts[u], starts[u + 1])
-            score(u, 1)
-        for s0 in range(early, N, GROUP):
-            part_group(s0)
-        for u in range(EARLY, len(WIDTHS)):
+        score(0, 1)
+        score_tile(0, 1)
+        score_tile(1, 1)
+        deal_both()
+        part_both()
+        for r in range(2, TILES):
+            for g in range(PASSES):
+                score_tile(r, g)
+        for u in range(1, len(UNITS)):
             for g in range(PASSES):
                 score(u, g)
         add_bias(0)
+        for t in range(2):
+            nc.scalar.activation(
+                started[:, t, :], tiles[t][:], mybir.ActivationFunctionType.Identity, bias=bias_col[0][:, t : t + 1]
+            )
+        page_max(0)
+        for t in range(2):
+            nc.vector.scalar_tensor_tensor(
+                folded[:, t, :], tiles[2 + t][:], bias_col[0][:, 2 + t : 3 + t], started[:, t, :], add, amax
+            )
+        back = bank("back", [P, 2, P], 7)
+        for t in range(2):
+            nc.tensor.transpose(back[:, t, :], folded[:, t, :], ident[:])
         add_bias(1)
-        page_max(0, starts[1])
         add_bias(2)
-        page_max(starts[1], starts[2])
-        add_bias(3)
-        add_bias(4)
-        page_max(starts[2], starts[3])
-        page_max(starts[3], N)
+        page_max(1)
+        page_max(2)
+        nc.vector.tensor_reduce(
+            best[:, LEAD // SEG : (LEAD + HALF) // SEG],
+            back[:].rearrange("p t (j c) -> p j t c", c=RUN),
+            mybir.AxisListType.XY,
+            amax,
+        )
         nc.vector.tensor_scalar_mul(result[:], best[:], weight[:])
         nc.sync.dma_start(out=out[0], in_=result[:])

@@ -21,10 +21,10 @@ HALF = 512
 PASSES = 2
 ROWS = 32
 SPLIT = 3456
-TILES = 4
-RUN = SEG // TILES
-LEAD = 256
-UNITS = [(0, LEAD), (LEAD + HALF, LEAD + HALF + P), (LEAD + HALF + P, N)]
+STEPS = 4
+RUN = SEG // STEPS
+CHAINS = 2
+WIDE = CHAINS * P
 HELP = 48
 
 FLOPS = 2 * 1024 * N * NQ
@@ -34,6 +34,7 @@ BYTES = P * T * 4 + 32 * T + 1024 * NQ * 4 + T * 4 + NQ * 4 + P * 64 * 2 + NQ * 
 def tile_attend_page_prior_kernel(tc, qT, k_words, k_scales, kb, pw, offs, out):
     nc = tc.nc
     add = mybir.AluOpType.add
+    mult = mybir.AluOpType.mult
     amax = mybir.AluOpType.max
     with ExitStack() as ctx:
         keep = ctx.enter_context(tc.tile_pool(name="keep", bufs=1))
@@ -53,9 +54,8 @@ def tile_attend_page_prior_kernel(tc, qT, k_words, k_scales, kb, pw, offs, out):
         scale_dealt = keep.tile([P, N], U8, name="scale_dealt", align_bytes=64)
         planes = keep.tile([P, PASSES * N], U8, name="planes", align_bytes=64)
         ident = keep.tile([P, P], F32, name="ident", align_bytes=64)
-        bias_col = [place("bias_col0", [P, 4], F32, 16448), keep.tile([P, 4], F32, name="bias_col1", tag="column1")]
         scale_pool = keep.tile([P, T + 4], U8, name="scale_pool", align_bytes=64)
-        q_raw = [place("q_raw0", [P, 4, NQ], F32, 0), place("q_raw1", [P, 4, NQ], F32, 16384)]
+        q_raw = [place("q_raw0", [P, 4, NQ], F32, 256), place("q_raw1", [P, 4, NQ], F32, 16384)]
 
         nc.sync.dma_start(offsets[:], offs)
         for g in range(PASSES):
@@ -81,12 +81,8 @@ def tile_attend_page_prior_kernel(tc, qT, k_words, k_scales, kb, pw, offs, out):
 
         nc.vector.tensor_copy(scale_got[:], scale_pool[:, 0:T].indirect(offsets[:]))
         nc.vector.tensor_copy(
-            scale_dealt[0:ROWS, LEAD : LEAD + HALF].bitcast(I32).rearrange("p (r j c) -> p j r c", r=TILES, c=RUN // 4),
-            scale_got[0:ROWS, LEAD : LEAD + HALF].bitcast(I32).rearrange("p (j r c) -> p j r c", r=TILES, c=RUN // 4),
-        )
-        nc.vector.tensor_copy(
-            scale_dealt[0:ROWS, :].bitcast(I32).rearrange("p (a n) -> p a n", a=4)[:, 0:4:3, :],
-            scale_got[0:ROWS, :].bitcast(I32).rearrange("p (a n) -> p a n", a=4)[:, 0:4:3, :],
+            scale_dealt[0:ROWS, :].bitcast(I32).rearrange("p (r j c) -> p j r c", r=STEPS, c=RUN // 4),
+            scale_got[0:ROWS, :].bitcast(I32).rearrange("p (j r c) -> p j r c", r=STEPS, c=RUN // 4),
         )
 
         def send_both(quad):
@@ -109,42 +105,31 @@ def tile_attend_page_prior_kernel(tc, qT, k_words, k_scales, kb, pw, offs, out):
             send_half(1, h)
             send_half(3, h)
 
-        bias_first = place("bias_first", [P, HALF], F32, 8192)
-        bias_second = place("bias_second", [P, HALF], F32, 2560)
-        bias_dealt = place("bias_dealt", [P, HALF], F32, 6144)
-        for h, s0 in enumerate((0, LEAD + HALF)):
+        turned = []
+        for h in range(CHAINS):
+            bias_got = keep.tile([P, HALF], F32, name="bias_got%d" % h)
+            bias_dealt = place("bias_dealt%d" % h, [P, HALF], F32, 6144 + 2048 * h)
             nc.scalar.activation(
-                bias_second[:, h * LEAD : (h + 1) * LEAD],
-                bias_pool[:].indirect(offsets[:, s0 // 16 : (s0 + LEAD) // 16]),
+                bias_got[:],
+                bias_pool[:].indirect(offsets[:, h * HALF // 16 : (h + 1) * HALF // 16]),
                 mybir.ActivationFunctionType.Copy,
             )
-        nc.scalar.activation(
-            bias_first[:],
-            bias_pool[:].indirect(offsets[:, LEAD // 16 : (LEAD + HALF) // 16]),
-            mybir.ActivationFunctionType.Copy,
-        )
-        nc.gpsimd.tensor_scalar(
-            bias_dealt[:].rearrange("p (r j c) -> p r j c", r=TILES, c=RUN),
-            bias_first[:].rearrange("p (j r c) -> p r j c", r=TILES, c=RUN),
-            1.0,
-            0.0,
-            mybir.AluOpType.mult,
-            add,
-        )
-        turned = [bank("turned%d" % h, [P, 4, P], h) for h in range(2)]
-        for b in range(4):
-            nc.tensor.transpose(turned[1][:, b, :], bias_second[:, b * P : (b + 1) * P], ident[:])
-        nc.scalar.copy(bias_col[1][:], turned[1][:, :, P - 1])
-        spread = bank("spread", [P, 4, P], 7)
-        for b in range(4):
-            nc.tensor.transpose(spread[:, b, :], bias_col[1][:, b : b + 1].to_broadcast([P, P]), ident[:])
-        for b in range(4):
-            nc.tensor.transpose(turned[0][:, b, :], bias_dealt[:, b * P : (b + 1) * P], ident[:])
+            dealing = (
+                bias_dealt[:].rearrange("p (r j c) -> p r j c", r=STEPS, c=RUN),
+                bias_got[:].rearrange("p (j r c) -> p r j c", r=STEPS, c=RUN),
+            )
+            if h == 0:
+                nc.gpsimd.tensor_scalar(*dealing, 1.0, 0.0, mult, add)
+            else:
+                nc.scalar.copy(*dealing)
+            turned.append(bank("turned%d" % h, [P, STEPS, P], 6 + h))
+            for r in range(STEPS):
+                nc.tensor.transpose(turned[h][:, r, :], bias_dealt[:, r * P : (r + 1) * P], ident[:])
 
-        weight = keep.tile([P, 1], F32, name="weight", tag="column1")
+        weight = place("weight", [P, 1], F32, 8192)
         nc.sync.dma_start(out=weight[:], in_=pw[0])
 
-        q_bf = [place("q_bf0", [P, NQ, 4], BF16, 3072), place("q_bf1", [P, NQ, 4], BF16, 4096)]
+        q_bf = [keep.tile([P, NQ, 4], BF16, name="q_bf0", align_bytes=64), place("q_bf1", [P, NQ, 4], BF16, 2048)]
 
         def rounding(g, w0, w1):
             return (
@@ -153,57 +138,37 @@ def tile_attend_page_prior_kernel(tc, qT, k_words, k_scales, kb, pw, offs, out):
             )
 
         nc.scalar.copy(*rounding(0, 0, NQ - HELP))
-        nc.gpsimd.tensor_scalar(*rounding(0, NQ - HELP, NQ), 1.0, 0.0, mybir.AluOpType.mult, add)
+        nc.gpsimd.tensor_scalar(*rounding(0, NQ - HELP, NQ), 1.0, 0.0, mult, add)
         nc.scalar.copy(*rounding(1, 0, NQ))
-        nc.scalar.copy(bias_col[0][:], turned[0][:, :, P - 1])
-        bias_rows = place("bias_rows", [P, HALF], F32, 16512)
-        nc.scalar.copy(bias_rows[:], spread[:].rearrange("p b n -> p (b n)"))
+        bias_col = [place("bias_col%d" % h, [P, STEPS], F32, 16448 + 64 * h) for h in range(CHAINS)]
+        for h in range(CHAINS):
+            nc.scalar.copy(bias_col[h][:], turned[h][:, :, P - 1])
 
         got = place("word_got", [P, N], U32, 20480)
         q_codes = keep.tile([P, PASSES * NQ], U32, name="q_codes", align_bytes=64)
         q_scales = keep.tile([P, PASSES * NQ], U8, name="q_scales", align_bytes=64)
-        before = place("parted_before", [P, 4 * HALF], U8, 1024)
-        after = place("parted_after", [P, 4 * HALF], U8, 14400)
+        early = [
+            [place("early%d_%d" % (r, g), [P, 2 * WIDE], U8, 2 * WIDE * (PASSES * r + g)) for g in range(PASSES)]
+            for r in range(2)
+        ]
+        late = [place("late0", [P, 4 * WIDE], U8, 15424), place("late1", [P, 4 * WIDE], U8, 17408)]
+        by_step = got[:].bitcast(U16).rearrange("p (j r c g) -> p r g j c", r=STEPS, c=RUN, g=PASSES)
 
-        def parted(g, s0, s1):
-            tile = before if s0 < HALF else after
-            first = s0 - s0 % LEAD
-            base = 2 * (first % HALF) + g * LEAD - first
-            return tile[:, 2 * (base + s0) : 2 * (base + s1)]
-
-        totals = keep.tile([P, HALF], F32, name="totals")
-        started = keep.tile([P, 2, NQ], F32, name="started")
-        folded = keep.tile([P, 2, NQ], F32, name="folded", align_bytes=64)
-        best = keep.tile([P, N // SEG], F32, name="best")
-        result = keep.tile([P, N // SEG], F32, name="result")
-        halves = got[:].bitcast(U16).rearrange("p (n g) -> p g n", g=PASSES)
-        tiles = {}
-        scores = {}
+        def parted(r, g):
+            if r < 2:
+                return early[r][g][:]
+            return late[r - 2][:, 2 * WIDE * g : 2 * WIDE * (g + 1)]
 
         def gather_words(s0, s1):
             nc.vector.tensor_copy(got[:, s0:s1], word_pool[:].bitcast(U32).indirect(offsets[:, s0 // 16 : s1 // 16]))
 
-        by_tile = halves[:, :, LEAD : LEAD + HALF].rearrange("p g (j r c) -> p g r j c", r=TILES, c=RUN)
+        def deal(r, g):
+            nc.vector.tensor_copy(parted(r, g).bitcast(U16).rearrange("p (j c) -> p j c", c=RUN), by_step[:, r, g, :, :])
 
-        def part(g):
-            nc.vector.tensor_copy(parted(g, 0, LEAD).bitcast(U16), halves[:, g, 0:LEAD])
-
-        def deal(g):
+        def deal_both(r):
             nc.vector.tensor_copy(
-                parted(g, LEAD, HALF).bitcast(U16).rearrange("p (r j c) -> p r j c", r=2, c=RUN),
-                by_tile[:, g, 0:2, :, :],
-            )
-
-        def deal_both():
-            nc.vector.tensor_copy(
-                after[:, 0 : 4 * LEAD].bitcast(U16).rearrange("p (g r j c) -> p g r j c", g=PASSES, r=2, c=RUN),
-                by_tile[:, :, 2:4, :, :],
-            )
-
-        def part_both():
-            nc.vector.tensor_copy(
-                after[:, 4 * LEAD : 8 * LEAD].bitcast(U16).rearrange("p (g n) -> p g n", g=PASSES),
-                halves[:, :, LEAD + HALF : N],
+                late[r - 2][:].bitcast(U16).rearrange("p (g j c) -> p g j c", g=PASSES, c=RUN),
+                by_step[:, r, :, :, :],
             )
 
         def quantise(g):
@@ -213,92 +178,66 @@ def tile_attend_page_prior_kernel(tc, qT, k_words, k_scales, kb, pw, offs, out):
                 in_=q_bf[g][:].rearrange("p w j -> p (w j)"),
             )
 
-        def score_tile(r, g):
-            s0 = LEAD + r * P
+        tiles = {}
+
+        def score(r, h, g):
             if g == 0:
-                tiles[r] = bank("tile%d" % r, [P, NQ], TILES - 1 - r)
+                tiles[r, h] = bank("tile%d_%d" % (r, h), [P, NQ], CHAINS * r + h)
+            s0 = g * N + r * WIDE + h * P
             nc.tensor.matmul_mx(
-                out=tiles[r][:],
-                lhsT=parted(g, s0, s0 + P).bitcast(FP4X4),
-                lhsT_scale=planes[:, g * N + s0 : g * N + s0 + P],
+                out=tiles[r, h][:],
+                lhsT=parted(r, g)[:, 2 * P * h : 2 * P * (h + 1)].bitcast(FP4X4),
+                lhsT_scale=planes[:, s0 : s0 + P],
                 rhs=q_codes[:, g * NQ : (g + 1) * NQ].bitcast(FP8X4),
                 rhs_scale=q_scales[:, g * NQ : (g + 1) * NQ],
                 start=(g == 0),
                 stop=(g == PASSES - 1),
             )
 
-        def score(u, g):
-            s0, s1 = UNITS[u]
-            if g == 0:
-                scores[u] = bank("scores%d" % u, [P, s1 - s0], TILES + u)
-            nc.tensor.matmul_mx(
-                out=scores[u][:],
-                lhsT=q_codes[:, g * NQ : (g + 1) * NQ].bitcast(FP8X4),
-                lhsT_scale=q_scales[:, g * NQ : (g + 1) * NQ],
-                rhs=parted(g, s0, s1).bitcast(FP4X4),
-                rhs_scale=planes[:, g * N + s0 : g * N + s1],
-                start=(g == 0),
-                stop=(g == PASSES - 1),
-            )
+        running = {}
 
-        def add_bias(u):
-            s0, s1 = (s - HALF * min(u, 1) for s in UNITS[u])
-            nc.vector.tensor_tensor(totals[:, s0:s1], scores[u][:], bias_rows[:, s0:s1], add)
-
-        def page_max(u):
-            s0, s1 = UNITS[u]
-            shift = HALF * min(u, 1)
-            nc.vector.tensor_reduce(
-                best[:, s0 // SEG : s1 // SEG],
-                totals[:, s0 - shift : s1 - shift].rearrange("p (j s) -> p j s", s=SEG),
-                mybir.AxisListType.X,
-                amax,
-            )
+        def fold(r, h):
+            running[r, h] = keep.tile([P, NQ], F32, name="running%d_%d" % (r, h), align_bytes=64)
+            bias = bias_col[h][:, r : r + 1]
+            if r == 0:
+                nc.scalar.activation(running[r, h][:], tiles[r, h][:], mybir.ActivationFunctionType.Identity, bias=bias)
+            else:
+                nc.vector.scalar_tensor_tensor(running[r, h][:], tiles[r, h][:], bias, running[r - 1, h][:], add, amax)
 
         gather_words(0, HALF)
         gather_words(HALF, N)
         quantise(0)
-        part(0)
-        score(0, 0)
-        deal(0)
-        score_tile(0, 0)
-        score_tile(1, 0)
-        part(1)
-        deal(1)
+        for r in range(2):
+            deal(r, 0)
+            for h in range(CHAINS):
+                score(r, h, 0)
+        for r in range(2):
+            deal(r, 1)
         quantise(1)
-        score(0, 1)
-        score_tile(0, 1)
-        score_tile(1, 1)
-        deal_both()
-        part_both()
-        for r in range(2, TILES):
-            for g in range(PASSES):
-                score_tile(r, g)
-        for u in range(1, len(UNITS)):
-            for g in range(PASSES):
-                score(u, g)
-        add_bias(0)
-        for t in range(2):
-            nc.scalar.activation(
-                started[:, t, :], tiles[t][:], mybir.ActivationFunctionType.Identity, bias=bias_col[0][:, t : t + 1]
+        for r in range(2):
+            for h in range(CHAINS):
+                score(r, h, 1)
+        for r in range(2, STEPS):
+            deal_both(r)
+        for r in range(2, STEPS):
+            for h in range(CHAINS):
+                for g in range(PASSES):
+                    score(r, h, g)
+        for r in range(STEPS):
+            for h in range(CHAINS):
+                fold(r, h)
+
+        best = keep.tile([P, N // SEG], F32, name="best")
+        result = keep.tile([P, N // SEG], F32, name="result")
+        pages = HALF // SEG
+        for h in range(CHAINS):
+            back = bank("back%d" % h, [P, P], h)
+            nc.tensor.transpose(back[:], running[STEPS - 1, h][:], ident[:])
+            nc.vector.tensor_reduce(
+                best[:, h * pages : (h + 1) * pages],
+                back[:].rearrange("p (j c) -> p j c", c=RUN),
+                mybir.AxisListType.X,
+                amax,
             )
-        page_max(0)
-        for t in range(2):
-            nc.vector.scalar_tensor_tensor(
-                folded[:, t, :], tiles[2 + t][:], bias_col[0][:, 2 + t : 3 + t], started[:, t, :], add, amax
-            )
-        back = bank("back", [P, 2, P], 7)
-        for t in range(2):
-            nc.tensor.transpose(back[:, t, :], folded[:, t, :], ident[:])
-        add_bias(1)
-        add_bias(2)
-        page_max(1)
-        page_max(2)
-        nc.vector.tensor_reduce(
-            best[:, LEAD // SEG : (LEAD + HALF) // SEG],
-            back[:].rearrange("p t (j c) -> p j t c", c=RUN),
-            mybir.AxisListType.XY,
-            amax,
-        )
         nc.vector.tensor_scalar_mul(result[:], best[:], weight[:])
         nc.sync.dma_start(out=out[0], in_=result[:])

@@ -21,10 +21,11 @@ HALF = 512
 PASSES = 2
 ROWS = 32
 SPLIT = 3456
-STEPS = 4
-RUN = SEG // STEPS
-CHAINS = 2
-WIDE = CHAINS * P
+PAIRS = 3
+RUN = SEG // 2
+WIDE = 2 * P
+TILED = PAIRS * WIDE
+UNITS = (N - TILED) // P
 HELP = 48
 
 FLOPS = 2 * 1024 * N * NQ
@@ -55,7 +56,7 @@ def tile_attend_page_prior_kernel(tc, qT, k_words, k_scales, kb, pw, offs, out):
         planes = keep.tile([P, PASSES * N], U8, name="planes", align_bytes=64)
         ident = keep.tile([P, P], F32, name="ident", align_bytes=64)
         scale_pool = keep.tile([P, T + 4], U8, name="scale_pool", align_bytes=64)
-        q_raw = [place("q_raw0", [P, 4, NQ], F32, 256), place("q_raw1", [P, 4, NQ], F32, 16384)]
+        q_raw = [place("q_raw0", [P, 4, NQ], F32, 768), place("q_raw1", [P, 4, NQ], F32, 16384)]
 
         nc.sync.dma_start(offsets[:], offs)
         for g in range(PASSES):
@@ -81,9 +82,10 @@ def tile_attend_page_prior_kernel(tc, qT, k_words, k_scales, kb, pw, offs, out):
 
         nc.vector.tensor_copy(scale_got[:], scale_pool[:, 0:T].indirect(offsets[:]))
         nc.vector.tensor_copy(
-            scale_dealt[0:ROWS, :].bitcast(I32).rearrange("p (r j c) -> p j r c", r=STEPS, c=RUN // 4),
-            scale_got[0:ROWS, :].bitcast(I32).rearrange("p (j r c) -> p j r c", r=STEPS, c=RUN // 4),
+            scale_dealt[0:ROWS, 0:TILED].bitcast(I32).rearrange("p (a r j c) -> p a j r c", a=PAIRS, r=2, c=RUN // 4),
+            scale_got[0:ROWS, 0:TILED].bitcast(I32).rearrange("p (a j r c) -> p a j r c", a=PAIRS, r=2, c=RUN // 4),
         )
+        nc.vector.tensor_copy(scale_dealt[0:ROWS, TILED:N].bitcast(I32), scale_got[0:ROWS, TILED:N].bitcast(I32))
 
         def send_both(quad):
             nc.sync.dma_start(
@@ -91,45 +93,65 @@ def tile_attend_page_prior_kernel(tc, qT, k_words, k_scales, kb, pw, offs, out):
                 in_=scale_dealt[8 * quad : 8 * quad + 8, :].bitcast(I32),
             )
 
-        def send_half(quad, h):
+        def send_part(quad, s0, s1):
             nc.sync.dma_start(
                 out=planes[32 * quad : 32 * quad + 4, :]
                 .bitcast(I32)
-                .rearrange("p (g n) -> p g n", g=PASSES)[:, :, h * HALF // 4 : (h + 1) * HALF // 4],
-                in_=scale_dealt[8 * quad : 8 * quad + 8, h * HALF : (h + 1) * HALF].bitcast(I32),
+                .rearrange("p (g n) -> p g n", g=PASSES)[:, :, s0 // 4 : s1 // 4],
+                in_=scale_dealt[8 * quad : 8 * quad + 8, s0:s1].bitcast(I32),
             )
 
         send_both(0)
         send_both(2)
-        for h in range(2):
-            send_half(1, h)
-            send_half(3, h)
+        for s0, s1 in ((0, TILED), (TILED, N)):
+            send_part(1, s0, s1)
+            send_part(3, s0, s1)
 
-        turned = []
-        for h in range(CHAINS):
-            bias_got = keep.tile([P, HALF], F32, name="bias_got%d" % h)
-            bias_dealt = place("bias_dealt%d" % h, [P, HALF], F32, 6144 + 2048 * h)
+        def gather_bias(tile, s0, s1):
             nc.scalar.activation(
-                bias_got[:],
-                bias_pool[:].indirect(offsets[:, h * HALF // 16 : (h + 1) * HALF // 16]),
-                mybir.ActivationFunctionType.Copy,
+                tile, bias_pool[:].indirect(offsets[:, s0 // 16 : s1 // 16]), mybir.ActivationFunctionType.Copy
             )
-            dealing = (
-                bias_dealt[:].rearrange("p (r j c) -> p r j c", r=STEPS, c=RUN),
-                bias_got[:].rearrange("p (j r c) -> p r j c", r=STEPS, c=RUN),
-            )
-            if h == 0:
-                nc.gpsimd.tensor_scalar(*dealing, 1.0, 0.0, mult, add)
-            else:
-                nc.scalar.copy(*dealing)
-            turned.append(bank("turned%d" % h, [P, STEPS, P], 6 + h))
-            for r in range(STEPS):
-                nc.tensor.transpose(turned[h][:, r, :], bias_dealt[:, r * P : (r + 1) * P], ident[:])
 
-        weight = place("weight", [P, 1], F32, 8192)
+        def dealing(tile, source, pairs):
+            return (
+                tile.rearrange("p (a r j c) -> p a r j c", a=pairs, r=2, c=RUN),
+                source.rearrange("p (a j r c) -> p a r j c", a=pairs, r=2, c=RUN),
+            )
+
+        bias_mixed = place("bias_mixed", [P, WIDE], F32, 4096)
+        bias_last = keep.tile([P, WIDE], F32, name="bias_last")
+        bias_first = keep.tile([P, HALF], F32, name="bias_first")
+        bias_dealt = place("bias_dealt", [P, HALF], F32, 6144)
+        gather_bias(bias_last[:], HALF, TILED)
+        units_got = keep.tile([P, WIDE], F32, name="units_got")
+        gather_bias(units_got[:], TILED, N)
+        gather_bias(bias_first[:], 0, HALF)
+        nc.gpsimd.tensor_scalar(
+            bias_mixed[:].rearrange("p (r j c) -> p r j c", r=2, c=RUN),
+            bias_last[:].rearrange("p (j r c) -> p r j c", r=2, c=RUN),
+            1.0,
+            0.0,
+            mult,
+            add,
+        )
+        nc.scalar.copy(*dealing(bias_dealt[:], bias_first[:], 2))
+        turned = [bank("turned%d" % h, [P, 4, P], 6 + h) for h in range(2)]
+        for u in range(UNITS):
+            nc.tensor.transpose(turned[1][:, 2 + u, :], units_got[:, u * P : (u + 1) * P], ident[:])
+        for r in range(2):
+            nc.tensor.transpose(turned[1][:, r, :], bias_mixed[:, r * P : (r + 1) * P], ident[:])
+        late_col = keep.tile([P, 4], F32, name="late_col")
+        nc.scalar.copy(late_col[:], turned[1][:, :, P - 1])
+        spread = bank("spread", [P, UNITS, P], 7)
+        for u in range(UNITS):
+            nc.tensor.transpose(spread[:, u, :], late_col[:, 2 + u : 3 + u].to_broadcast([P, P]), ident[:])
+        for b in range(4):
+            nc.tensor.transpose(turned[0][:, b, :], bias_dealt[:, b * P : (b + 1) * P], ident[:])
+
+        weight = place("weight", [P, 1], F32, 6144)
         nc.sync.dma_start(out=weight[:], in_=pw[0])
 
-        q_bf = [keep.tile([P, NQ, 4], BF16, name="q_bf0", align_bytes=64), place("q_bf1", [P, NQ, 4], BF16, 2048)]
+        q_bf = [place("q_bf0", [P, NQ, 4], BF16, 4096), place("q_bf1", [P, NQ, 4], BF16, 0)]
 
         def rounding(g, w0, w1):
             return (
@@ -140,35 +162,34 @@ def tile_attend_page_prior_kernel(tc, qT, k_words, k_scales, kb, pw, offs, out):
         nc.scalar.copy(*rounding(0, 0, NQ - HELP))
         nc.gpsimd.tensor_scalar(*rounding(0, NQ - HELP, NQ), 1.0, 0.0, mult, add)
         nc.scalar.copy(*rounding(1, 0, NQ))
-        bias_col = [place("bias_col%d" % h, [P, STEPS], F32, 16448 + 64 * h) for h in range(CHAINS)]
-        for h in range(CHAINS):
-            nc.scalar.copy(bias_col[h][:], turned[h][:, :, P - 1])
+        early_col = place("early_col", [P, 4], F32, 16448)
+        nc.scalar.copy(early_col[:], turned[0][:, :, P - 1])
+        bias_rows = place("bias_rows", [P, WIDE], F32, 16512)
+        nc.scalar.copy(bias_rows[:], spread[:].rearrange("p b n -> p (b n)"))
 
         got = place("word_got", [P, N], U32, 20480)
         q_codes = keep.tile([P, PASSES * NQ], U32, name="q_codes", align_bytes=64)
         q_scales = keep.tile([P, PASSES * NQ], U8, name="q_scales", align_bytes=64)
-        early = [
-            [place("early%d_%d" % (r, g), [P, 2 * WIDE], U8, 2 * WIDE * (PASSES * r + g)) for g in range(PASSES)]
-            for r in range(2)
-        ]
-        late = [place("late0", [P, 4 * WIDE], U8, 15424), place("late1", [P, 4 * WIDE], U8, 17408)]
-        by_step = got[:].bitcast(U16).rearrange("p (j r c g) -> p r g j c", r=STEPS, c=RUN, g=PASSES)
+        first = [place("first%d" % a, [P, 2 * WIDE], U8, 1024 + 2 * WIDE * a) for a in range(PAIRS)]
+        second = place("second", [P, 4 * WIDE], U8, 2560)
+        third = place("third", [P, 2 * WIDE], U8, 15936)
+        plain = place("plain", [P, 4 * WIDE], U8, 17536)
+        by_tile = got[:, 0:TILED].bitcast(U16).rearrange("p (a j r c g) -> p g a r j c", a=PAIRS, r=2, c=RUN, g=PASSES)
+        halves = got[:].bitcast(U16).rearrange("p (n g) -> p g n", g=PASSES)
 
-        def parted(r, g):
-            if r < 2:
-                return early[r][g][:]
-            return late[r - 2][:, 2 * WIDE * g : 2 * WIDE * (g + 1)]
+        def parted(a, g):
+            if g == 0:
+                return first[a][:]
+            if a < 2:
+                return second[:, 2 * WIDE * a : 2 * WIDE * (a + 1)]
+            return third[:]
 
         def gather_words(s0, s1):
             nc.vector.tensor_copy(got[:, s0:s1], word_pool[:].bitcast(U32).indirect(offsets[:, s0 // 16 : s1 // 16]))
 
-        def deal(r, g):
-            nc.vector.tensor_copy(parted(r, g).bitcast(U16).rearrange("p (j c) -> p j c", c=RUN), by_step[:, r, g, :, :])
-
-        def deal_both(r):
+        def deal(a, g):
             nc.vector.tensor_copy(
-                late[r - 2][:].bitcast(U16).rearrange("p (g j c) -> p g j c", g=PASSES, c=RUN),
-                by_step[:, r, :, :, :],
+                parted(a, g).bitcast(U16).rearrange("p (r j c) -> p r j c", r=2, c=RUN), by_tile[:, g, a, :, :, :]
             )
 
         def quantise(g):
@@ -179,14 +200,15 @@ def tile_attend_page_prior_kernel(tc, qT, k_words, k_scales, kb, pw, offs, out):
             )
 
         tiles = {}
+        scores = {}
 
-        def score(r, h, g):
+        def score_tile(a, r, g):
             if g == 0:
-                tiles[r, h] = bank("tile%d_%d" % (r, h), [P, NQ], CHAINS * r + h)
-            s0 = g * N + r * WIDE + h * P
+                tiles[a, r] = bank("tile%d_%d" % (a, r), [P, NQ], 2 * a + r)
+            s0 = g * N + a * WIDE + r * P
             nc.tensor.matmul_mx(
-                out=tiles[r, h][:],
-                lhsT=parted(r, g)[:, 2 * P * h : 2 * P * (h + 1)].bitcast(FP4X4),
+                out=tiles[a, r][:],
+                lhsT=parted(a, g)[:, 2 * P * r : 2 * P * (r + 1)].bitcast(FP4X4),
                 lhsT_scale=planes[:, s0 : s0 + P],
                 rhs=q_codes[:, g * NQ : (g + 1) * NQ].bitcast(FP8X4),
                 rhs_scale=q_scales[:, g * NQ : (g + 1) * NQ],
@@ -194,48 +216,77 @@ def tile_attend_page_prior_kernel(tc, qT, k_words, k_scales, kb, pw, offs, out):
                 stop=(g == PASSES - 1),
             )
 
-        running = {}
-
-        def fold(r, h):
-            running[r, h] = keep.tile([P, NQ], F32, name="running%d_%d" % (r, h), align_bytes=64)
-            bias = bias_col[h][:, r : r + 1]
-            if r == 0:
-                nc.scalar.activation(running[r, h][:], tiles[r, h][:], mybir.ActivationFunctionType.Identity, bias=bias)
-            else:
-                nc.vector.scalar_tensor_tensor(running[r, h][:], tiles[r, h][:], bias, running[r - 1, h][:], add, amax)
+        def score_unit(u, g):
+            if g == 0:
+                scores[u] = bank("scores%d" % u, [P, P], 6 + u)
+            s0 = g * N + TILED + u * P
+            c0 = 2 * (g * WIDE + u * P)
+            nc.tensor.matmul_mx(
+                out=scores[u][:],
+                lhsT=q_codes[:, g * NQ : (g + 1) * NQ].bitcast(FP8X4),
+                lhsT_scale=q_scales[:, g * NQ : (g + 1) * NQ],
+                rhs=plain[:, c0 : c0 + 2 * P].bitcast(FP4X4),
+                rhs_scale=planes[:, s0 : s0 + P],
+                start=(g == 0),
+                stop=(g == PASSES - 1),
+            )
 
         gather_words(0, HALF)
         gather_words(HALF, N)
         quantise(0)
-        for r in range(2):
-            deal(r, 0)
-            for h in range(CHAINS):
-                score(r, h, 0)
-        for r in range(2):
-            deal(r, 1)
+        for a in range(PAIRS):
+            deal(a, 0)
+            for r in range(2):
+                score_tile(a, r, 0)
+        nc.vector.tensor_copy(
+            second[:].bitcast(U16).rearrange("p (a r j c) -> p a r j c", a=2, r=2, c=RUN), by_tile[:, 1, 0:2, :, :, :]
+        )
         quantise(1)
+        deal(2, 1)
+        nc.vector.tensor_copy(
+            plain[:].bitcast(U16).rearrange("p (g n) -> p g n", g=PASSES), halves[:, :, TILED:N]
+        )
         for r in range(2):
-            for h in range(CHAINS):
-                score(r, h, 1)
-        for r in range(2, STEPS):
-            deal_both(r)
-        for r in range(2, STEPS):
-            for h in range(CHAINS):
-                for g in range(PASSES):
-                    score(r, h, g)
-        for r in range(STEPS):
-            for h in range(CHAINS):
-                fold(r, h)
+            for a in range(PAIRS):
+                score_tile(a, r, 1)
+        for u in range(UNITS):
+            for g in range(PASSES):
+                score_unit(u, g)
 
+        def column(a, r):
+            if a < 2:
+                return early_col[:, 2 * a + r : 2 * a + r + 1]
+            return late_col[:, r : r + 1]
+
+        started = keep.tile([P, PAIRS, NQ], F32, name="started")
+        folded = keep.tile([P, PAIRS, NQ], F32, name="folded", align_bytes=64)
+        totals = keep.tile([P, WIDE], F32, name="totals")
         best = keep.tile([P, N // SEG], F32, name="best")
         result = keep.tile([P, N // SEG], F32, name="result")
-        pages = HALF // SEG
-        for h in range(CHAINS):
-            back = bank("back%d" % h, [P, P], h)
-            nc.tensor.transpose(back[:], running[STEPS - 1, h][:], ident[:])
+        for a in range(PAIRS):
+            nc.scalar.activation(
+                started[:, a, :], tiles[a, 0][:], mybir.ActivationFunctionType.Identity, bias=column(a, 0)
+            )
+        for a in range(PAIRS):
+            nc.vector.scalar_tensor_tensor(folded[:, a, :], tiles[a, 1][:], column(a, 1), started[:, a, :], add, amax)
+        back = [bank("back%d" % a, [P, P], 2 * a) for a in range(PAIRS)]
+        for a in range(PAIRS):
+            nc.tensor.transpose(back[a][:], folded[:, a, :], ident[:])
+        for u in range(UNITS):
+            nc.vector.tensor_tensor(totals[:, u * P : (u + 1) * P], scores[u][:], bias_rows[:, u * P : (u + 1) * P], add)
+        for u in range(UNITS):
+            page = (TILED + u * P) // SEG
             nc.vector.tensor_reduce(
-                best[:, h * pages : (h + 1) * pages],
-                back[:].rearrange("p (j c) -> p j c", c=RUN),
+                best[:, page : page + P // SEG],
+                totals[:, u * P : (u + 1) * P].rearrange("p (j s) -> p j s", s=SEG),
+                mybir.AxisListType.X,
+                amax,
+            )
+        for a in range(PAIRS):
+            page = a * WIDE // SEG
+            nc.vector.tensor_reduce(
+                best[:, page : page + WIDE // SEG],
+                back[a][:].rearrange("p (j c) -> p j c", c=RUN),
                 mybir.AxisListType.X,
                 amax,
             )

@@ -171,25 +171,37 @@ def tile_attend_page_prior_kernel(tc, qT, k_words, k_scales, kb, pw, offs, out):
         q_codes = keep.tile([P, PASSES * NQ], U32, name="q_codes", align_bytes=64)
         q_scales = keep.tile([P, PASSES * NQ], U8, name="q_scales", align_bytes=64)
         first = [place("first%d" % a, [P, 2 * WIDE], U8, 1024 + 2 * WIDE * a) for a in range(PAIRS)]
-        second = place("second", [P, 4 * WIDE], U8, 2560)
-        third = place("third", [P, 2 * WIDE], U8, 15936)
+        second = [
+            place("second0", [P, 2 * PAIRS * P], U8, 2560),
+            place("second1", [P, 2 * PAIRS * P], U8, 15680),
+        ]
         plain = place("plain", [P, 4 * WIDE], U8, 17536)
         by_tile = got[:, 0:TILED].bitcast(U16).rearrange("p (a j r c g) -> p g a r j c", a=PAIRS, r=2, c=RUN, g=PASSES)
+        by_step = got[:, 0:TILED].bitcast(U16).rearrange("p (j r c g) -> p g r j c", r=2, c=RUN, g=PASSES)
         halves = got[:].bitcast(U16).rearrange("p (n g) -> p g n", g=PASSES)
 
-        def parted(a, g):
+        def parted(a, r, g):
             if g == 0:
-                return first[a][:]
-            if a < 2:
-                return second[:, 2 * WIDE * a : 2 * WIDE * (a + 1)]
-            return third[:]
+                return first[a][:, 2 * P * r : 2 * P * (r + 1)]
+            return second[r][:, 2 * P * a : 2 * P * (a + 1)]
 
         def gather_words(s0, s1):
             nc.vector.tensor_copy(got[:, s0:s1], word_pool[:].bitcast(U32).indirect(offsets[:, s0 // 16 : s1 // 16]))
 
-        def deal(a, g):
+        def deal_first(a):
             nc.vector.tensor_copy(
-                parted(a, g).bitcast(U16).rearrange("p (r j c) -> p r j c", r=2, c=RUN), by_tile[:, g, a, :, :, :]
+                first[a][:].bitcast(U16).rearrange("p (r j c) -> p r j c", r=2, c=RUN), by_tile[:, 0, a, :, :, :]
+            )
+
+        def deal_second(r):
+            nc.vector.tensor_copy(
+                second[r][:].bitcast(U16).rearrange("p (j c) -> p j c", c=RUN), by_step[:, 1, r, :, :]
+            )
+
+        def deal_tile(r):
+            nc.vector.tensor_copy(
+                first[0][:, 2 * P * r : 2 * P * (r + 1)].bitcast(U16).rearrange("p (j c) -> p j c", c=RUN),
+                by_tile[:, 0, 0, r, :, :],
             )
 
         def quantise(g):
@@ -208,7 +220,7 @@ def tile_attend_page_prior_kernel(tc, qT, k_words, k_scales, kb, pw, offs, out):
             s0 = g * N + a * WIDE + r * P
             nc.tensor.matmul_mx(
                 out=tiles[a, r][:],
-                lhsT=parted(a, g)[:, 2 * P * r : 2 * P * (r + 1)].bitcast(FP4X4),
+                lhsT=parted(a, r, g).bitcast(FP4X4),
                 lhsT_scale=planes[:, s0 : s0 + P],
                 rhs=q_codes[:, g * NQ : (g + 1) * NQ].bitcast(FP8X4),
                 rhs_scale=q_scales[:, g * NQ : (g + 1) * NQ],
@@ -233,16 +245,17 @@ def tile_attend_page_prior_kernel(tc, qT, k_words, k_scales, kb, pw, offs, out):
 
         gather_words(0, HALF)
         gather_words(HALF, N)
+        deal_tile(0)
         quantise(0)
+        deal_tile(1)
         for a in range(PAIRS):
-            deal(a, 0)
+            if a > 0:
+                deal_first(a)
             for r in range(2):
                 score_tile(a, r, 0)
-        nc.vector.tensor_copy(
-            second[:].bitcast(U16).rearrange("p (a r j c) -> p a r j c", a=2, r=2, c=RUN), by_tile[:, 1, 0:2, :, :, :]
-        )
+        deal_second(0)
         quantise(1)
-        deal(2, 1)
+        deal_second(1)
         nc.vector.tensor_copy(
             plain[:].bitcast(U16).rearrange("p (g n) -> p g n", g=PASSES), halves[:, :, TILED:N]
         )

from contextlib import ExitStack

import concourse.mybir as mybir
from concourse.masks import make_identity

F32 = mybir.dt.float32
BF16 = mybir.dt.bfloat16
I32 = mybir.dt.int32
U32 = mybir.dt.uint32
U16 = mybir.dt.uint16
U8 = mybir.dt.uint8
FP8X4 = mybir.dt.float8_e4m3fn_x4
FP4X4 = mybir.dt.float4_e2m1fn_x4

P = 128
T = 4096
N = 1024
NQ = 128
SEG = 32
HALF = 512
PASSES = 2
ROWS = 32
SPLIT = 3456
PAIRS = 3
RUN = SEG // 2
WIDE = 2 * P
TILED = PAIRS * WIDE
UNITS = (N - TILED) // P
HELP = 48

FLOPS = 2 * 1024 * N * NQ
BYTES = P * T * 4 + 32 * T + 1024 * NQ * 4 + T * 4 + NQ * 4 + P * 64 * 2 + NQ * 32 * 4


def tile_attend_page_prior_kernel(tc, qT, k_words, k_scales, kb, pw, offs, out):
    nc = tc.nc
    add = mybir.AluOpType.add
    mult = mybir.AluOpType.mult
    amax = mybir.AluOpType.max
    with ExitStack() as ctx:
        keep = ctx.enter_context(tc.tile_pool(name="keep", bufs=1))
        placed = ctx.enter_context(tc.tile_pool(name="placed", bufs=1))
        psum = ctx.enter_context(tc.psum_pool(name="psum", bufs=1))

        def place(name, shape, dtype, offset):
            return placed.tile(shape, dtype, name=name, offset=offset, align_bytes=64)

        def bank(name, shape, number):
            return psum.tile(shape, F32, name=name, tag="bank%d" % number)

        offsets = keep.tile([P, N // 16], U16, name="offsets")
        word_pool = keep.tile([P, T], I32, name="word_pool", align_bytes=64)
        bias_pool = keep.tile([P, T], F32, name="bias_pool", align_bytes=64)
        scale_got = place("scale_got", [P, N], U8, 20480)
        scale_dealt = keep.tile([P, N], U8, name="scale_dealt", align_bytes=64)
        planes = keep.tile([P, PASSES * N], U8, name="planes", align_bytes=64)
        ident = keep.tile([P, P], F32, name="ident", align_bytes=64)
        scale_pool = keep.tile([P, T + 4], U8, name="scale_pool", align_bytes=64)
        q_raw = [place("q_raw0", [P, 4, NQ], F32, 768), place("q_raw1", [P, 4, NQ], F32, 16384)]

        nc.sync.dma_start(offsets[:], offs)
        for g in range(PASSES):
            nc.sync.dma_start(out=scale_pool[g:ROWS:PASSES, 0:T].bitcast(I32), in_=k_scales[g].bitcast(I32))
        nc.scalar.dma_start(out=bias_pool[P - 1 : P, :], in_=kb[0:1, :])
        nc.sync.dma_start(out=word_pool[:], in_=k_words[0].rearrange("p t b -> p (t b)").bitcast(I32))
        q_rows = qT[0].rearrange("(g p j) w -> g p j w", g=PASSES, j=4)
        for g in range(PASSES):
            nc.sync.dma_start(out=q_raw[g][:], in_=q_rows[g])

        spare = keep.tile([P, 16], F32, name="spare")
        nc.vector.memset(spare[:, 0:1], 0.0)
        nc.scalar.copy(spare[:, 8:9], spare[:, 0:1])

        nc.gpsimd.memset(bias_pool[0 : P - 1, 0:SPLIT], 0.0)
        middle = (SPLIT + T) // 2 + 1
        nc.vector.memset(bias_pool[0 : P - 1, SPLIT:middle], 0.0)
        nc.vector.memset(bias_pool[0 : P - 1, middle:T], 0.0)
        make_identity(nc, ident[:])
        nc.gpsimd.memset(planes[:].bitcast(I32), 0)
        nc.vector.memset(scale_pool[32:64, :].bitcast(I32), 0)
        nc.vector.memset(scale_pool[64:P, :].bitcast(I32), 0)

        nc.vector.tensor_copy(scale_got[:], scale_pool[:, 0:T].indirect(offsets[:]))
        nc.vector.tensor_copy(
            scale_dealt[0:ROWS, 0:TILED].bitcast(I32).rearrange("p (a r j c) -> p a j r c", a=PAIRS, r=2, c=RUN // 4),
            scale_got[0:ROWS, 0:TILED].bitcast(I32).rearrange("p (a j r c) -> p a j r c", a=PAIRS, r=2, c=RUN // 4),
        )
        nc.vector.tensor_copy(scale_dealt[0:ROWS, TILED:N].bitcast(I32), scale_got[0:ROWS, TILED:N].bitcast(I32))

        def send_both(quad):
            nc.sync.dma_start(
                out=planes[32 * quad : 32 * quad + 4, :].bitcast(I32),
                in_=scale_dealt[8 * quad : 8 * quad + 8, :].bitcast(I32),
            )

        def send_part(quad, s0, s1):
            nc.sync.dma_start(
                out=planes[32 * quad : 32 * quad + 4, :]
                .bitcast(I32)
                .rearrange("p (g n) -> p g n", g=PASSES)[:, :, s0 // 4 : s1 // 4],
                in_=scale_dealt[8 * quad : 8 * quad + 8, s0:s1].bitcast(I32),
            )

        send_both(0)
        send_both(2)
        for s0, s1 in ((0, TILED), (TILED, N)):
            send_part(1, s0, s1)
            send_part(3, s0, s1)

        def gather_bias(tile, s0, s1):
            nc.scalar.activation(
                tile, bias_pool[:].indirect(offsets[:, s0 // 16 : s1 // 16]), mybir.ActivationFunctionType.Copy
            )

        def dealing(tile, source, pairs):
            return (
                tile.rearrange("p (a r j c) -> p a r j c", a=pairs, r=2, c=RUN),
                source.rearrange("p (a j r c) -> p a r j c", a=pairs, r=2, c=RUN),
            )

        bias_mixed = place("bias_mixed", [P, WIDE], F32, 4096)
        bias_last = keep.tile([P, WIDE], F32, name="bias_last")
        bias_first = keep.tile([P, HALF], F32, name="bias_first")
        bias_dealt = place("bias_dealt", [P, HALF], F32, 6144)
        gather_bias(bias_last[:], HALF, TILED)
        units_got = keep.tile([P, WIDE], F32, name="units_got")
        gather_bias(units_got[:], TILED, N)
        gather_bias(bias_first[:], 0, HALF)
        nc.gpsimd.tensor_scalar(
            bias_mixed[:].rearrange("p (r j c) -> p r j c", r=2, c=RUN),
            bias_last[:].rearrange("p (j r c) -> p r j c", r=2, c=RUN),
            1.0,
            0.0,
            mult,
            add,
        )
        nc.scalar.copy(*dealing(bias_dealt[:], bias_first[:], 2))
        turned = [bank("turned%d" % h, [P, 4, P], 6 + h) for h in range(2)]
        for u in range(UNITS):
            nc.tensor.transpose(turned[1][:, 2 + u, :], units_got[:, u * P : (u + 1) * P], ident[:])
        for r in range(2):
            nc.tensor.transpose(turned[1][:, r, :], bias_mixed[:, r * P : (r + 1) * P], ident[:])
        late_col = keep.tile([P, 4], F32, name="late_col")
        nc.scalar.copy(late_col[:], turned[1][:, :, P - 1])
        spread = bank("spread", [P, UNITS, P], 7)
        for u in range(UNITS):
            nc.tensor.transpose(spread[:, u, :], late_col[:, 2 + u : 3 + u].to_broadcast([P, P]), ident[:])
        for b in range(4):
            nc.tensor.transpose(turned[0][:, b, :], bias_dealt[:, b * P : (b + 1) * P], ident[:])

        weight = place("weight", [P, 1], F32, 6144)
        nc.sync.dma_start(out=weight[:], in_=pw[0])

        q_bf = [place("q_bf0", [P, NQ, 4], BF16, 4096), place("q_bf1", [P, NQ, 4], BF16, 0)]

        def rounding(g, w0, w1):
            return (
                q_bf[g][:, w0:w1, :].rearrange("p (c i) j -> p c j i", i=4),
                q_raw[g][:, :, w0:w1].rearrange("p j (c i) -> p c j i", i=4),
            )

        nc.scalar.copy(*rounding(0, 0, NQ - HELP))
        nc.gpsimd.tensor_scalar(*rounding(0, NQ - HELP, NQ), 1.0, 0.0, mult, add)
        nc.scalar.copy(*rounding(1, 0, NQ))
        early_col = place("early_col", [P, 4], F32, 16448)
        nc.scalar.copy(early_col[:], turned[0][:, :, P - 1])
        bias_rows = place("bias_rows", [P, WIDE], F32, 16512)
        nc.scalar.copy(bias_rows[:], spread[:].rearrange("p b n -> p (b n)"))

        got = place("word_got", [P, N], U32, 20480)
        q_codes = keep.tile([P, PASSES * NQ], U32, name="q_codes", align_bytes=64)
        q_scales = keep.tile([P, PASSES * NQ], U8, name="q_scales", align_bytes=64)
        first = [place("first%d" % a, [P, 2 * WIDE], U8, 1024 + 2 * WIDE * a) for a in range(PAIRS)]
        second = [
            place("second0", [P, 2 * PAIRS * P], U8, 2560),
            place("second1", [P, 2 * PAIRS * P], U8, 15680),
        ]
        plain = place("plain", [P, 4 * WIDE], U8, 17536)
        by_tile = got[:, 0:TILED].bitcast(U16).rearrange("p (a j r c g) -> p g a r j c", a=PAIRS, r=2, c=RUN, g=PASSES)
        by_step = got[:, 0:TILED].bitcast(U16).rearrange("p (j r c g) -> p g r j c", r=2, c=RUN, g=PASSES)
        halves = got[:].bitcast(U16).rearrange("p (n g) -> p g n", g=PASSES)

        def parted(a, r, g):
            if g == 0:
                return first[a][:, 2 * P * r : 2 * P * (r + 1)]
            return second[r][:, 2 * P * a : 2 * P * (a + 1)]

        def gather_words(s0, s1):
            nc.vector.tensor_copy(got[:, s0:s1], word_pool[:].bitcast(U32).indirect(offsets[:, s0 // 16 : s1 // 16]))

        def deal_first(a):
            nc.vector.tensor_copy(
                first[a][:].bitcast(U16).rearrange("p (r j c) -> p r j c", r=2, c=RUN), by_tile[:, 0, a, :, :, :]
            )

        def deal_second(r):
            nc.vector.tensor_copy(
                second[r][:].bitcast(U16).rearrange("p (j c) -> p j c", c=RUN), by_step[:, 1, r, :, :]
            )

        def deal_tile(r):
            nc.vector.tensor_copy(
                first[0][:, 2 * P * r : 2 * P * (r + 1)].bitcast(U16).rearrange("p (j c) -> p j c", c=RUN),
                by_tile[:, 0, 0, r, :, :],
            )

        def quantise(g):
            nc.vector.quantize_mx(
                out=q_codes[:, g * NQ : (g + 1) * NQ].bitcast(FP8X4),
                scales=q_scales[:, g * NQ : (g + 1) * NQ],
                in_=q_bf[g][:].rearrange("p w j -> p (w j)"),
            )

        tiles = {}
        scores = {}

        def score_tile(a, r, g):
            if g == 0:
                tiles[a, r] = bank("tile%d_%d" % (a, r), [P, NQ], 2 * a + r)
            s0 = g * N + a * WIDE + r * P
            nc.tensor.matmul_mx(
                out=tiles[a, r][:],
                lhsT=parted(a, r, g).bitcast(FP4X4),
                lhsT_scale=planes[:, s0 : s0 + P],
                rhs=q_codes[:, g * NQ : (g + 1) * NQ].bitcast(FP8X4),
                rhs_scale=q_scales[:, g * NQ : (g + 1) * NQ],
                start=(g == 0),
                stop=(g == PASSES - 1),
            )

        def score_unit(u, g):
            if g == 0:
                scores[u] = bank("scores%d" % u, [P, P], 6 + u)
            s0 = g * N + TILED + u * P
            c0 = 2 * (g * WIDE + u * P)
            nc.tensor.matmul_mx(
                out=scores[u][:],
                lhsT=q_codes[:, g * NQ : (g + 1) * NQ].bitcast(FP8X4),
                lhsT_scale=q_scales[:, g * NQ : (g + 1) * NQ],
                rhs=plain[:, c0 : c0 + 2 * P].bitcast(FP4X4),
                rhs_scale=planes[:, s0 : s0 + P],
                start=(g == 0),
                stop=(g == PASSES - 1),
            )

        gather_words(0, HALF)
        gather_words(HALF, N)
        deal_tile(0)
        quantise(0)
        deal_tile(1)
        for a in range(PAIRS):
            if a > 0:
                deal_first(a)
            for r in range(2):
                score_tile(a, r, 0)
        deal_second(0)
        quantise(1)
        deal_second(1)
        nc.vector.tensor_copy(
            plain[:].bitcast(U16).rearrange("p (g n) -> p g n", g=PASSES), halves[:, :, TILED:N]
        )
        for r in range(2):
            for a in range(PAIRS):
                score_tile(a, r, 1)
        for u in range(UNITS):
            for g in range(PASSES):
                score_unit(u, g)

        def column(a, r):
            if a < 2:
                return early_col[:, 2 * a + r : 2 * a + r + 1]
            return late_col[:, r : r + 1]

        started = keep.tile([P, PAIRS, NQ], F32, name="started")
        folded = keep.tile([P, PAIRS, NQ], F32, name="folded", align_bytes=64)
        totals = keep.tile([P, WIDE], F32, name="totals")
        best = keep.tile([P, N // SEG], F32, name="best")
        result = keep.tile([P, N // SEG], F32, name="result")
        for a in range(PAIRS):
            nc.scalar.activation(
                started[:, a, :], tiles[a, 0][:], mybir.ActivationFunctionType.Identity, bias=column(a, 0)
            )
        for a in range(PAIRS):
            nc.vector.scalar_tensor_tensor(folded[:, a, :], tiles[a, 1][:], column(a, 1), started[:, a, :], add, amax)
        back = [bank("back%d" % a, [P, P], 2 * a) for a in range(PAIRS)]
        for a in range(PAIRS):
            nc.tensor.transpose(back[a][:], folded[:, a, :], ident[:])
        for u in range(UNITS):
            nc.vector.tensor_tensor(totals[:, u * P : (u + 1) * P], scores[u][:], bias_rows[:, u * P : (u + 1) * P], add)
        for u in range(UNITS):
            page = (TILED + u * P) // SEG
            nc.vector.tensor_reduce(
                best[:, page : page + P // SEG],
                totals[:, u * P : (u + 1) * P].rearrange("p (j s) -> p j s", s=SEG),
                mybir.AxisListType.X,
                amax,
            )
        for a in range(PAIRS):
            page = a * WIDE // SEG
            nc.vector.tensor_reduce(
                best[:, page : page + WIDE // SEG],
                back[a][:].rearrange("p (j c) -> p j c", c=RUN),
                mybir.AxisListType.X,
                amax,
            )
        nc.vector.tensor_scalar_mul(result[:], best[:], weight[:])
        nc.sync.dma_start(out=out[0], in_=result[:])
